import numpy as np
import ml_dtypes


def mxq(x, axis, fmt="e4m3"):
    dtype, down = {"e4m3": (ml_dtypes.float8_e4m3fn, 7), "e5m2": (ml_dtypes.float8_e5m2, 14)}[fmt]
    v = np.moveaxis(np.asarray(x, np.float32).astype(ml_dtypes.bfloat16).astype(np.float64), axis, -1)
    blocks = v.reshape(v.shape[:-1] + (-1, 32))
    amax = np.abs(blocks).max(-1, keepdims=True)
    byte = np.maximum(np.where(amax > 0, np.frexp(amax)[1] - 1 + 127, 0) - down, 1)
    scale = np.exp2(byte - 127.0)
    codes = (blocks / scale).astype(np.float32).astype(dtype).astype(np.float64)
    return np.moveaxis((codes * scale).reshape(v.shape), -1, axis)


WIDE = False


def mx_kscale(k):
    if not WIDE:
        return np.ones(k)
    levels = np.array([18, -18])
    if k % 512:
        return np.exp2(np.random.permutation(np.resize(levels, k // 32))).repeat(32)
    a = np.empty((k // 512, 16))
    for p in range(k // 512):
        a[p, :8] = np.random.permutation(np.resize(levels, 8))
        for g in range(8):
            far = levels[np.abs(levels - a[p, g]) >= 10]
            a[p, g + 8] = far[np.random.randint(len(far))]
    return np.exp2(a.ravel()).repeat(32)


def f64(x):
    return np.asarray(x).astype(np.float64)


def striped(idx):
    return np.tile(np.asarray(idx).reshape(-1, 16).T, (8, 1)).astype(np.uint16)


def unstriped(offs):
    return offs[:16].T.reshape(-1).astype(np.int64)


N, C, D, R = 1024, 2048, 512, 256


def eight(codes):
    return np.concatenate([codes[h].reshape(-1, 16).T for h in range(8)]).astype(np.uint16)


def uneight(offs):
    return np.stack([offs[16 * h:16 * h + 16].T.reshape(-1) for h in range(8)]).astype(np.int64)


def setup_inputs():
    n = np.random.standard_normal
    s = mx_kscale(D)[:, None]
    u = mx_kscale(N)
    grid = lambda x: np.round(x * 32) / 32
    return {
        "xT": (n((D, R)) * (1.0 / np.sqrt(D)) * s).astype(np.float32),
        "cb": (grid(n((D, C))) / s).astype(np.float32),
        "norm": np.tile(np.random.randint(32, 129, N) / 64.0 / u, (128, 1)).astype(np.float32),
        "ts": np.tile(np.random.uniform(0.5, 1.5, N) * u, (128, 1)).astype(np.float32),
        "y": np.random.randint(0, 2, (R, N)).astype(np.float32),
        "wt": (np.random.uniform(0.5, 1.5, (R, 1)) * 1.0 / np.sqrt(N)).astype(np.float32),
        "offs": eight(np.random.randint(0, C, (8, N))),
    }


def reference(xT, cb, norm, ts, y, wt, offs):
    code = uneight(offs)
    k = np.concatenate([f64(cb)[64 * h:64 * h + 64][:, code[h]] for h in range(8)]) * f64(norm)[:1]
    a = f64(ts)[:1] * (mxq(f64(xT), 0, "e4m3").T @ mxq(k, 0, "e4m3"))
    g = f64(wt) * (1.0 / (1.0 + np.exp(-a)) - f64(y))
    h = f64(ts)[:1] * g
    return mxq(h, 1, "e5m2") @ mxq(k, 1, "e4m3").T

@@ -1,0 +1,246 @@
+from contextlib import ExitStack
+
+import concourse.mybir as mybir
+from concourse.masks import make_identity
+
+N, C, D, R = 1024, 2048, 512, 256
+FLOPS = 2 * 2 * N * D * R
+
+F32 = mybir.dt.float32
+BF16 = mybir.dt.bfloat16
+U32 = mybir.dt.uint32
+U16 = mybir.dt.uint16
+U8 = mybir.dt.uint8
+E4M3 = mybir.dt.float8_e4m3fn_x4
+E5M2 = mybir.dt.float8_e5m2_x4
+MULT = mybir.AluOpType.mult
+SUBTRACT = mybir.AluOpType.subtract
+COPY = mybir.ActivationFunctionType.Copy
+SIGMOID = mybir.ActivationFunctionType.Sigmoid
+
+P = 128
+PACK = 4
+PASS = P * PACK
+PASSES = N // PASS
+ROW_TILES = R // P
+LIST_ROWS = 16
+
+
+def tile_attend_gpq_nce_x_kernel(tc, xT, cb, norm, ts, y, wt, offs, out):
+    nc = tc.nc
+    with ExitStack() as ctx:
+        sb = ctx.enter_context(tc.tile_pool(name="sb", bufs=1))
+        ps = ctx.enter_context(tc.psum_pool(name="ps", bufs=1))
+
+        def bank(index, name):
+            return ps.tile([P, PASS], F32, name=name, tag="bank%d" % index)
+
+        def tiles(name, count, shape, dtype):
+            return [sb.tile(shape, dtype, name="%s%d" % (name, i), align_bytes=64) for i in range(count)]
+
+        offsets = sb.tile([P, N // LIST_ROWS], U16, name="offsets")
+        norm_sb = tiles("norm_sb", PASSES, [P, PASS], F32)
+        planes = tiles("planes", PACK, [P, C], F32)
+        x_raw = sb.tile([P, PACK, R], F32, name="x_raw")
+        y_sb = tiles("y_sb", PASSES, [P, ROW_TILES, PASS], F32)
+        ts_col = sb.tile([P, PASSES, PACK], F32, name="ts_col")
+        norm_col = sb.tile([P, PASSES, PACK], F32, name="norm_col")
+        wt_col = sb.tile([P, 2], F32, name="wt_col")
+
+        cb_planes = cb.rearrange("(p t) c -> t p c", t=PACK)
+        y_rows = y.rearrange("(j m) n -> m j n", m=P)
+        nc.scalar.dma_start(norm_col[:], norm[0:1, :].rearrange("o (g s t) -> s (o g) t", g=PASSES, t=PACK))
+        nc.sync.dma_start(planes[0][:], cb_planes[0])
+        nc.sync.dma_start(offsets[:], offs)
+        nc.scalar.dma_start(wt_col[:], wt.rearrange("(p e) o -> p (e o)", e=2))
+        nc.scalar.dma_start(ts_col[:], ts[0:1, :].rearrange("o (g s t) -> s (o g) t", g=PASSES, t=PACK))
+        for t in range(1, PACK - 1):
+            nc.sync.dma_start(planes[t][:], cb_planes[t])
+        nc.sync.dma_start(x_raw[:], xT.rearrange("(p t) r -> p t r", t=PACK))
+        nc.sync.dma_start(planes[PACK - 1][:], cb_planes[PACK - 1])
+        for g in range(PASSES):
+            nc.sync.dma_start(y_sb[g][:], y_rows[:, :, g * PASS : (g + 1) * PASS])
+
+        identity = sb.tile([P, P], F32, name="identity")
+        make_identity(nc, identity[:])
+        warm_in = sb.tile([P, 1], F32, name="warm_in")
+        warm = sb.tile([P, 1], F32, name="warm")
+        nc.vector.memset(warm_in[:], 0.0)
+        nc.scalar.activation(warm[:], warm_in[:], SIGMOID)
+
+        for g in range(PASSES):
+            spread = bank(2 + g, "norm_spread")
+            for t in range(PACK):
+                nc.tensor.transpose(spread[:, t * P : (t + 1) * P], norm_col[:, g, t : t + 1].to_broadcast([P, P]), identity[:])
+            nc.scalar.copy(
+                norm_sb[g][:].rearrange("q (s t) -> q s t", t=PACK), spread[:].rearrange("q (t s) -> q s t", t=PACK)
+            )
+
+        wt_bank = bank(0, "wt_bank")
+        for e in range(2):
+            nc.tensor.transpose(wt_bank[:, e * P : (e + 1) * P], wt_col[:, e : e + 1].to_broadcast([P, P]), identity[:])
+        wt_row = wt_bank[:, 0:R].rearrange("q (e j k) -> q j k e", e=2, j=ROW_TILES)
+        weight = tiles("weight", PASSES, [P, ROW_TILES, PACK, P], F32)
+        for g in range(PASSES):
+            for t in range(PACK):
+                nc.scalar.activation(
+                    weight[g][:, :, t, :].rearrange("q j (k e) -> q j k e", e=2), wt_row, COPY, scale=ts_col[:, g, t : t + 1]
+                )
+
+        gathered = [tiles("gathered%d_" % g, 2, [P, 2, PASS], F32) for g in range(PASSES)]
+        k_bf = tiles("k_bf", PASSES, [P, PACK, P, PACK], BF16)
+        k_codes = tiles("k_codes", PASSES, [P, PASS], U32)
+        k_scales = tiles("k_scales", PASSES, [P, PASS], U8)
+        kt_bf = [tiles("kt_bf%d_" % g, 2, [P, D // 2, PACK], BF16) for g in range(PASSES)]
+        kt_codes = tiles("kt_codes", PASSES, [P, D], U32)
+        kt_scales = tiles("kt_scales", PASSES, [P, D], U8)
+        x_bf = sb.tile([P, R, PACK], BF16, name="x_bf", align_bytes=64)
+        x_codes = sb.tile([P, R], U32, name="x_codes", align_bytes=64)
+        x_scales = sb.tile([P, R], U8, name="x_scales", align_bytes=64)
+        sig = tiles("sig", PASSES, [P, ROW_TILES, PACK, P], F32)
+        diff = [tiles("diff%d_" % g, ROW_TILES, [P, PACK, P], F32) for g in range(PASSES)]
+        h_bf = [tiles("h_bf%d_" % g, ROW_TILES, [P, P, PACK], BF16) for g in range(PASSES)]
+        h_codes = [tiles("h_codes%d_" % g, ROW_TILES, [P, P], U32) for g in range(PASSES)]
+        h_scales = [tiles("h_scales%d_" % g, ROW_TILES, [P, P], U8) for g in range(PASSES)]
+        result = tiles("result", ROW_TILES, [P, D], F32)
+
+        def gather(td, g):
+            columns = PASS // LIST_ROWS
+            window = planes[td][:].indirect(offsets[:, g * columns : (g + 1) * columns])
+            nc.vector.tensor_tensor(gathered[g][td // 2][:, td % 2, :], window, norm_sb[g][:], MULT)
+
+        def round_k(g, u):
+            nc.scalar.copy(
+                k_bf[g][:, :, :, 2 * u : 2 * u + 2].rearrange("p t s e -> p s e t"),
+                gathered[g][u][:].rearrange("p e (s t) -> p s e t", t=PACK),
+            )
+
+        def turn_k(g, u, index):
+            turned = bank(index, "k_turned")
+            words = k_bf[g][:].rearrange("p t s d -> p (t s d)").bitcast(F32)
+            for t in range(PACK):
+                nc.tensor.transpose(turned[:, t * P : (t + 1) * P], words[:, 2 * P * t + u : 2 * P * (t + 1) : 2], identity[:])
+            nc.scalar.copy(kt_bf[g][u][:], turned[:].bitcast(BF16).rearrange("s (t c) -> s c t", t=PACK))
+
+        def quantize(codes, scales, values, fmt):
+            nc.vector.quantize_mx(out=codes.bitcast(fmt), scales=scales, in_=values)
+
+        def quantize_kt(g, u):
+            half = slice(u * D // 2, (u + 1) * D // 2)
+            quantize(kt_codes[g][:, half], kt_scales[g][:, half], kt_bf[g][u][:].rearrange("s c t -> s (c t)"), E4M3)
+
+        def quantize_k(g):
+            quantize(k_codes[g][:], k_scales[g][:], k_bf[g][:].rearrange("p t s d -> p (t s d)"), E4M3)
+
+        def turn_y(g, first_bank):
+            banks = []
+            for j in range(ROW_TILES):
+                turned = bank(first_bank + j, "y_turned")
+                for t in range(PACK):
+                    nc.tensor.transpose(turned[:, t * P : (t + 1) * P], y_sb[g][:, j, t:PASS:PACK], identity[:])
+                banks.append(turned)
+            return banks
+
+        def scores(g, first_bank):
+            for b in range(2):
+                acc = bank(first_bank + b, "score")
+                for t in (2 * b, 2 * b + 1):
+                    cols = slice(t * P, (t + 1) * P)
+                    nc.tensor.matmul_mx(
+                        out=acc[:, (t % 2) * R : (t % 2 + 1) * R],
+                        lhsT=k_codes[g][:, cols].bitcast(E4M3),
+                        lhsT_scale=k_scales[g][:, cols],
+                        rhs=x_codes[:].bitcast(E4M3),
+                        rhs_scale=x_scales[:],
+                        start=True,
+                        stop=True,
+                    )
+                for t in (2 * b, 2 * b + 1):
+                    nc.scalar.activation(
+                        sig[g][:, :, t, :],
+                        acc[:, (t % 2) * R : (t % 2 + 1) * R].rearrange("s (j m) -> s j m", m=P),
+                        SIGMOID,
+                        scale=ts_col[:, g, t : t + 1],
+                    )
+
+        def residual(g, y_banks):
+            for j in range(ROW_TILES):
+                nc.vector.tensor_tensor(
+                    diff[g][j][:].rearrange("s t m -> s (t m)"),
+                    sig[g][:, j, :, :].rearrange("s t m -> s (t m)"),
+                    y_banks[j][:],
+                    SUBTRACT,
+                )
+
+        def weigh(g, j):
+            nc.vector.tensor_tensor(
+                h_bf[g][j][:].rearrange("s (c i) t -> s c t i", i=4),
+                diff[g][j][:].rearrange("s t (c i) -> s c t i", i=4),
+                weight[g][:, j, :, :].rearrange("s t (c i) -> s c t i", i=4),
+                MULT,
+            )
+
+        def quantize_h(g, j):
+            quantize(h_codes[g][j][:], h_scales[g][j][:], h_bf[g][j][:].rearrange("s m t -> s (m t)"), E5M2)
+
+        def gradient(g, j, acc):
+            nc.tensor.matmul_mx(
+                out=acc[:],
+                lhsT=h_codes[g][j][:].bitcast(E5M2),
+                lhsT_scale=h_scales[g][j][:],
+                rhs=kt_codes[g][:].bitcast(E4M3),
+                rhs_scale=kt_scales[g][:],
+                start=(g == 0),
+                stop=(g == PASSES - 1),
+            )
+
+        gather(0, 0)
+        gather(0, 1)
+        gather(1, 0)
+        round_k(0, 0)
+        turn_k(0, 0, 1)
+        gather(1, 1)
+        round_k(1, 0)
+        turn_k(1, 0, 0)
+        gather(2, 0)
+        gather(3, 0)
+        round_k(0, 1)
+        gather(2, 1)
+        gather(3, 1)
+        round_k(1, 1)
+        quantize_k(0)
+        nc.scalar.copy(
+            x_bf[:].rearrange("p (c i) t -> p c t i", i=4), x_raw[:].rearrange("p t (c i) -> p c t i", i=4)
+        )
+        quantize(x_codes[:], x_scales[:], x_bf[:].rearrange("p r t -> p (r t)"), E4M3)
+        scores(0, 2)
+        quantize_k(1)
+        quantize_kt(0, 0)
+        quantize_kt(1, 0)
+        y_banks0 = turn_y(0, 4)
+        scores(1, 0)
+        y_banks1 = turn_y(1, 6)
+        residual(0, y_banks0)
+        turn_k(0, 1, 4)
+        turn_k(1, 1, 5)
+        for j in range(ROW_TILES):
+            weigh(0, j)
+        for j in range(ROW_TILES):
+            quantize_h(0, j)
+        residual(1, y_banks1)
+        quantize_kt(0, 1)
+        sums = [bank(2 + j, "sums%d" % j) for j in range(ROW_TILES)]
+        for j in range(ROW_TILES):
+            gradient(0, j, sums[j])
+        weigh(1, 0)
+        quantize_kt(1, 1)
+        quantize_h(1, 0)
+        weigh(1, 1)
+        quantize_h(1, 1)
+        for j in range(ROW_TILES):
+            gradient(1, j, sums[j])
+            nc.scalar.copy(
+                result[j][:].rearrange("m (p u e) -> m p u e", u=2, e=2),
+                sums[j][:].rearrange("m (u p e) -> m p u e", u=2, e=2),
+            )
+            nc.sync.dma_start(out[j * P : (j + 1) * P, :], result[j][:])

@@ -49,15 +49,14 @@ def tile_attend_gpq_nce_x_kernel(tc, xT, cb, norm, ts, y, wt, offs, out):
 
         cb_planes = cb.rearrange("(p t) c -> t p c", t=PACK)
         y_rows = y.rearrange("(j m) n -> m j n", m=P)
-        nc.scalar.dma_start(norm_col[:], norm[0:1, :].rearrange("o (g s t) -> s (o g) t", g=PASSES, t=PACK))
+        nc.sync.dma_start(norm_col[:], norm[0:1, :].rearrange("o (g s t) -> s (o g) t", g=PASSES, t=PACK))
         nc.sync.dma_start(planes[0][:], cb_planes[0])
         nc.sync.dma_start(offsets[:], offs)
-        nc.scalar.dma_start(wt_col[:], wt.rearrange("(p e) o -> p (e o)", e=2))
-        nc.scalar.dma_start(ts_col[:], ts[0:1, :].rearrange("o (g s t) -> s (o g) t", g=PASSES, t=PACK))
-        for t in range(1, PACK - 1):
+        nc.sync.dma_start(wt_col[:], wt.rearrange("(p e) o -> p (e o)", e=2))
+        nc.sync.dma_start(ts_col[:], ts[0:1, :].rearrange("o (g s t) -> s (o g) t", g=PASSES, t=PACK))
+        for t in range(1, PACK):
             nc.sync.dma_start(planes[t][:], cb_planes[t])
         nc.sync.dma_start(x_raw[:], xT.rearrange("(p t) r -> p t r", t=PACK))
-        nc.sync.dma_start(planes[PACK - 1][:], cb_planes[PACK - 1])
         for g in range(PASSES):
             nc.sync.dma_start(y_sb[g][:], y_rows[:, :, g * PASS : (g + 1) * PASS])
 
@@ -69,36 +68,38 @@ def tile_attend_gpq_nce_x_kernel(tc, xT, cb, norm, ts, y, wt, offs, out):
         nc.scalar.activation(warm[:], warm_in[:], SIGMOID)
 
         for g in range(PASSES):
-            spread = bank(2 + g, "norm_spread")
+            spread = bank(g, "norm_spread")
             for t in range(PACK):
                 nc.tensor.transpose(spread[:, t * P : (t + 1) * P], norm_col[:, g, t : t + 1].to_broadcast([P, P]), identity[:])
             nc.scalar.copy(
                 norm_sb[g][:].rearrange("q (s t) -> q s t", t=PACK), spread[:].rearrange("q (t s) -> q s t", t=PACK)
             )
 
-        wt_bank = bank(0, "wt_bank")
-        for e in range(2):
-            nc.tensor.transpose(wt_bank[:, e * P : (e + 1) * P], wt_col[:, e : e + 1].to_broadcast([P, P]), identity[:])
-        wt_row = wt_bank[:, 0:R].rearrange("q (e j k) -> q j k e", e=2, j=ROW_TILES)
-        weight = tiles("weight", PASSES, [P, ROW_TILES, PACK, P], F32)
-        for g in range(PASSES):
-            for t in range(PACK):
-                nc.scalar.activation(
-                    weight[g][:, :, t, :].rearrange("q j (k e) -> q j k e", e=2), wt_row, COPY, scale=ts_col[:, g, t : t + 1]
-                )
+        weight = tiles("weight", PASSES, [P, PACK, R], F32)
 
-        gathered = [tiles("gathered%d_" % g, 2, [P, 2, PASS], F32) for g in range(PASSES)]
-        k_bf = tiles("k_bf", PASSES, [P, PACK, P, PACK], BF16)
+        def make_weight(index):
+            wt_bank = bank(index, "wt_bank")
+            for e in range(2):
+                nc.tensor.transpose(wt_bank[:, e * P : (e + 1) * P], wt_col[:, e : e + 1].to_broadcast([P, P]), identity[:])
+            wt_row = wt_bank[:, 0:R].rearrange("q (e k) -> q k e", e=2)
+            for g in range(PASSES):
+                for t in range(PACK):
+                    nc.scalar.activation(
+                        weight[g][:, t, :].rearrange("q (k e) -> q k e", e=2), wt_row, COPY, scale=ts_col[:, g, t : t + 1]
+                    )
+
+        gathered = tiles("gathered", PASSES, [P, PACK, PASS], F32)
+        k_bf = [tiles("k_bf%d_" % g, 2, [P, 2, P, PACK], BF16) for g in range(PASSES)]
         k_codes = tiles("k_codes", PASSES, [P, PASS], U32)
         k_scales = tiles("k_scales", PASSES, [P, PASS], U8)
-        kt_bf = [tiles("kt_bf%d_" % g, 2, [P, D // 2, PACK], BF16) for g in range(PASSES)]
+        kt_bf = [tiles("kt_bf%d_" % g, 2, [P, 2, P, PACK], BF16) for g in range(PASSES)]
         kt_codes = tiles("kt_codes", PASSES, [P, D], U32)
         kt_scales = tiles("kt_scales", PASSES, [P, D], U8)
         x_bf = sb.tile([P, R, PACK], BF16, name="x_bf", align_bytes=64)
         x_codes = sb.tile([P, R], U32, name="x_codes", align_bytes=64)
         x_scales = sb.tile([P, R], U8, name="x_scales", align_bytes=64)
-        sig = tiles("sig", PASSES, [P, ROW_TILES, PACK, P], F32)
-        diff = [tiles("diff%d_" % g, ROW_TILES, [P, PACK, P], F32) for g in range(PASSES)]
+        sig = tiles("sig", PASSES, [P, PACK, R], F32)
+        diff = tiles("diff", PASSES, [P, PACK, R], F32)
         h_bf = [tiles("h_bf%d_" % g, ROW_TILES, [P, P, PACK], BF16) for g in range(PASSES)]
         h_codes = [tiles("h_codes%d_" % g, ROW_TILES, [P, P], U32) for g in range(PASSES)]
         h_scales = [tiles("h_scales%d_" % g, ROW_TILES, [P, P], U8) for g in range(PASSES)]
@@ -107,76 +108,70 @@ def tile_attend_gpq_nce_x_kernel(tc, xT, cb, norm, ts, y, wt, offs, out):
         def gather(td, g):
             columns = PASS // LIST_ROWS
             window = planes[td][:].indirect(offsets[:, g * columns : (g + 1) * columns])
-            nc.vector.tensor_tensor(gathered[g][td // 2][:, td % 2, :], window, norm_sb[g][:], MULT)
+            nc.vector.tensor_tensor(gathered[g][:, td, :], window, norm_sb[g][:], MULT)
 
-        def round_k(g, u):
-            nc.scalar.copy(
-                k_bf[g][:, :, :, 2 * u : 2 * u + 2].rearrange("p t s e -> p s e t"),
-                gathered[g][u][:].rearrange("p e (s t) -> p s e t", t=PACK),
+        def round_k(g, b, copy):
+            copy(
+                k_bf[g][b][:].rearrange("p t s d -> p s d t"),
+                gathered[g][:].rearrange("p d (s t) -> p s d t", t=PACK)[:, :, :, 2 * b : 2 * b + 2],
             )
 
-        def turn_k(g, u, index):
+        def turn_k(td, g, index):
             turned = bank(index, "k_turned")
-            words = k_bf[g][:].rearrange("p t s d -> p (t s d)").bitcast(F32)
             for t in range(PACK):
-                nc.tensor.transpose(turned[:, t * P : (t + 1) * P], words[:, 2 * P * t + u : 2 * P * (t + 1) : 2], identity[:])
-            nc.scalar.copy(kt_bf[g][u][:], turned[:].bitcast(BF16).rearrange("s (t c) -> s c t", t=PACK))
+                nc.tensor.transpose(turned[:, t * P : (t + 1) * P], gathered[g][:, td, t:PASS:PACK], identity[:])
+            nc.scalar.copy(kt_bf[g][td // 2][:, td % 2], turned[:].rearrange("s (t p) -> s p t", t=PACK))
 
         def quantize(codes, scales, values, fmt):
             nc.vector.quantize_mx(out=codes.bitcast(fmt), scales=scales, in_=values)
 
         def quantize_kt(g, u):
             half = slice(u * D // 2, (u + 1) * D // 2)
-            quantize(kt_codes[g][:, half], kt_scales[g][:, half], kt_bf[g][u][:].rearrange("s c t -> s (c t)"), E4M3)
+            quantize(kt_codes[g][:, half], kt_scales[g][:, half], kt_bf[g][u][:].rearrange("s e p t -> s (e p t)"), E4M3)
 
-        def quantize_k(g):
-            quantize(k_codes[g][:], k_scales[g][:], k_bf[g][:].rearrange("p t s d -> p (t s d)"), E4M3)
+        def quantize_k(g, b):
+            cols = slice(2 * b * P, 2 * (b + 1) * P)
+            quantize(k_codes[g][:, cols], k_scales[g][:, cols], k_bf[g][b][:].rearrange("p t s d -> p (t s d)"), E4M3)
 
-        def turn_y(g, first_bank):
-            banks = []
-            for j in range(ROW_TILES):
-                turned = bank(first_bank + j, "y_turned")
-                for t in range(PACK):
-                    nc.tensor.transpose(turned[:, t * P : (t + 1) * P], y_sb[g][:, j, t:PASS:PACK], identity[:])
-                banks.append(turned)
-            return banks
+        def turn_y(g, b, index):
+            turned = bank(index, "y_turned")
+            for t in (2 * b, 2 * b + 1):
+                for j in range(ROW_TILES):
+                    first = (t % 2) * R + j * P
+                    nc.tensor.transpose(turned[:, first : first + P], y_sb[g][:, j, t:PASS:PACK], identity[:])
+            return turned
 
-        def scores(g, first_bank):
-            for b in range(2):
-                acc = bank(first_bank + b, "score")
-                for t in (2 * b, 2 * b + 1):
-                    cols = slice(t * P, (t + 1) * P)
-                    nc.tensor.matmul_mx(
-                        out=acc[:, (t % 2) * R : (t % 2 + 1) * R],
-                        lhsT=k_codes[g][:, cols].bitcast(E4M3),
-                        lhsT_scale=k_scales[g][:, cols],
-                        rhs=x_codes[:].bitcast(E4M3),
-                        rhs_scale=x_scales[:],
-                        start=True,
-                        stop=True,
-                    )
-                for t in (2 * b, 2 * b + 1):
-                    nc.scalar.activation(
-                        sig[g][:, :, t, :],
-                        acc[:, (t % 2) * R : (t % 2 + 1) * R].rearrange("s (j m) -> s j m", m=P),
-                        SIGMOID,
-                        scale=ts_col[:, g, t : t + 1],
-                    )
-
-        def residual(g, y_banks):
-            for j in range(ROW_TILES):
-                nc.vector.tensor_tensor(
-                    diff[g][j][:].rearrange("s t m -> s (t m)"),
-                    sig[g][:, j, :, :].rearrange("s t m -> s (t m)"),
-                    y_banks[j][:],
-                    SUBTRACT,
+        def scores(g, b, index):
+            acc = bank(index, "score")
+            for t in (2 * b, 2 * b + 1):
+                cols = slice(t * P, (t + 1) * P)
+                nc.tensor.matmul_mx(
+                    out=acc[:, (t % 2) * R : (t % 2 + 1) * R],
+                    lhsT=k_codes[g][:, cols].bitcast(E4M3),
+                    lhsT_scale=k_scales[g][:, cols],
+                    rhs=x_codes[:].bitcast(E4M3),
+                    rhs_scale=x_scales[:],
+                    start=True,
+                    stop=True,
                 )
+            for t in (2 * b, 2 * b + 1):
+                nc.scalar.activation(
+                    sig[g][:, t, :], acc[:, (t % 2) * R : (t % 2 + 1) * R], SIGMOID, scale=ts_col[:, g, t : t + 1]
+                )
+
+        def residual(g, b, y_turned):
+            nc.vector.tensor_tensor(
+                diff[g][:, 2 * b : 2 * b + 2, :].rearrange("s t r -> s (t r)"),
+                sig[g][:, 2 * b : 2 * b + 2, :].rearrange("s t r -> s (t r)"),
+                y_turned[:],
+                SUBTRACT,
+            )
 
         def weigh(g, j):
             nc.vector.tensor_tensor(
                 h_bf[g][j][:].rearrange("s (c i) t -> s c t i", i=4),
-                diff[g][j][:].rearrange("s t (c i) -> s c t i", i=4),
-                weight[g][:, j, :, :].rearrange("s t (c i) -> s c t i", i=4),
+                diff[g][:, :, j * P : (j + 1) * P].rearrange("s t (c i) -> s c t i", i=4),
+                weight[g][:, :, j * P : (j + 1) * P].rearrange("s t (c i) -> s c t i", i=4),
                 MULT,
             )
 
@@ -194,42 +189,50 @@ def tile_attend_gpq_nce_x_kernel(tc, xT, cb, norm, ts, y, wt, offs, out):
                 stop=(g == PASSES - 1),
             )
 
-        gather(0, 0)
-        gather(0, 1)
-        gather(1, 0)
-        round_k(0, 0)
-        turn_k(0, 0, 1)
-        gather(1, 1)
-        round_k(1, 0)
-        turn_k(1, 0, 0)
+        for td in range(PACK - 2):
+            for g in range(PASSES):
+                gather(td, g)
         gather(2, 0)
         gather(3, 0)
-        round_k(0, 1)
+        round_k(0, 0, nc.scalar.copy)
+        round_k(0, 1, nc.scalar.copy)
         gather(2, 1)
+        nc.vector.tensor_copy(x_bf[:].rearrange("p (c i) t -> p c t i", i=4), x_raw[:].rearrange("p t (c i) -> p c t i", i=4))
         gather(3, 1)
-        round_k(1, 1)
-        quantize_k(0)
-        nc.scalar.copy(
-            x_bf[:].rearrange("p (c i) t -> p c t i", i=4), x_raw[:].rearrange("p t (c i) -> p c t i", i=4)
-        )
+        turn_k(0, 0, 3)
+        turn_k(0, 1, 4)
+        make_weight(2)
+        turn_k(1, 0, 5)
+        turn_k(1, 1, 6)
+        turn_k(2, 0, 7)
+        turn_k(2, 1, 0)
+        quantize_k(0, 0)
         quantize(x_codes[:], x_scales[:], x_bf[:].rearrange("p r t -> p (r t)"), E4M3)
-        scores(0, 2)
-        quantize_k(1)
+        round_k(1, 1, nc.vector.tensor_copy)
+        quantize_k(0, 1)
+        y_banks0 = [turn_y(0, b, 5 + b) for b in range(2)]
+        scores(0, 0, 1)
+        scores(0, 1, 2)
+        round_k(1, 0, nc.scalar.copy)
+        quantize_k(1, 1)
+        quantize_k(1, 0)
+        scores(1, 1, 4)
+        scores(1, 0, 3)
+        for b in range(2):
+            residual(0, b, y_banks0[b])
+        y_banks1 = [turn_y(1, 1, 7), turn_y(1, 0, 1)]
+        turn_k(3, 0, 5)
+        turn_k(3, 1, 6)
         quantize_kt(0, 0)
         quantize_kt(1, 0)
-        y_banks0 = turn_y(0, 4)
-        scores(1, 0)
-        y_banks1 = turn_y(1, 6)
-        residual(0, y_banks0)
-        turn_k(0, 1, 4)
-        turn_k(1, 1, 5)
         for j in range(ROW_TILES):
             weigh(0, j)
+        for b in range(2):
+            residual(1, 1 - b, y_banks1[b])
         for j in range(ROW_TILES):
             quantize_h(0, j)
-        residual(1, y_banks1)
         quantize_kt(0, 1)
-        sums = [bank(2 + j, "sums%d" % j) for j in range(ROW_TILES)]
+        sums = [bank(2 * j, "sums%d" % j) for j in range(ROW_TILES)]
         for j in range(ROW_TILES):
             gradient(0, j, sums[j])
         weigh(1, 0)
@@ -240,7 +243,6 @@ def tile_attend_gpq_nce_x_kernel(tc, xT, cb, norm, ts, y, wt, offs, out):
         for j in range(ROW_TILES):
             gradient(1, j, sums[j])
             nc.scalar.copy(
-                result[j][:].rearrange("m (p u e) -> m p u e", u=2, e=2),
-                sums[j][:].rearrange("m (u p e) -> m p u e", u=2, e=2),
+                result[j][:].rearrange("m (p d) -> m p d", d=PACK), sums[j][:].rearrange("m (d p) -> m p d", d=PACK)
             )
             nc.sync.dma_start(out[j * P : (j + 1) * P, :], result[j][:])

@@ -100,9 +100,9 @@ def tile_attend_gpq_nce_x_kernel(tc, xT, cb, norm, ts, y, wt, offs, out):
         x_scales = sb.tile([P, R], U8, name="x_scales", align_bytes=64)
         sig = tiles("sig", PASSES, [P, PACK, R], F32)
         diff = tiles("diff", PASSES, [P, PACK, R], F32)
-        h_bf = [tiles("h_bf%d_" % g, ROW_TILES, [P, P, PACK], BF16) for g in range(PASSES)]
-        h_codes = [tiles("h_codes%d_" % g, ROW_TILES, [P, P], U32) for g in range(PASSES)]
-        h_scales = [tiles("h_scales%d_" % g, ROW_TILES, [P, P], U8) for g in range(PASSES)]
+        h_bf = tiles("h_bf", PASSES, [P, R, PACK], BF16)
+        h_codes = tiles("h_codes", PASSES, [P, R], U32)
+        h_scales = tiles("h_scales", PASSES, [P, R], U8)
         result = tiles("result", ROW_TILES, [P, D], F32)
 
         def gather(td, g):
@@ -167,22 +167,22 @@ def tile_attend_gpq_nce_x_kernel(tc, xT, cb, norm, ts, y, wt, offs, out):
                 SUBTRACT,
             )
 
-        def weigh(g, j):
+        def weigh(g, rows):
             nc.vector.tensor_tensor(
-                h_bf[g][j][:].rearrange("s (c i) t -> s c t i", i=4),
-                diff[g][:, :, j * P : (j + 1) * P].rearrange("s t (c i) -> s c t i", i=4),
-                weight[g][:, :, j * P : (j + 1) * P].rearrange("s t (c i) -> s c t i", i=4),
+                h_bf[g][:, rows, :].rearrange("s (c i) t -> s c t i", i=4),
+                diff[g][:, :, rows].rearrange("s t (c i) -> s c t i", i=4),
+                weight[g][:, :, rows].rearrange("s t (c i) -> s c t i", i=4),
                 MULT,
             )
 
-        def quantize_h(g, j):
-            quantize(h_codes[g][j][:], h_scales[g][j][:], h_bf[g][j][:].rearrange("s m t -> s (m t)"), E5M2)
+        def quantize_h(g, rows):
+            quantize(h_codes[g][:, rows], h_scales[g][:, rows], h_bf[g][:, rows, :].rearrange("s m t -> s (m t)"), E5M2)
 
         def gradient(g, j, acc):
             nc.tensor.matmul_mx(
                 out=acc[:],
-                lhsT=h_codes[g][j][:].bitcast(E5M2),
-                lhsT_scale=h_scales[g][j][:],
+                lhsT=h_codes[g][:, j * P : (j + 1) * P].bitcast(E5M2),
+                lhsT_scale=h_scales[g][:, j * P : (j + 1) * P],
                 rhs=kt_codes[g][:].bitcast(E4M3),
                 rhs_scale=kt_scales[g][:],
                 start=(g == 0),
@@ -195,10 +195,10 @@ def tile_attend_gpq_nce_x_kernel(tc, xT, cb, norm, ts, y, wt, offs, out):
         gather(2, 0)
         gather(3, 0)
         round_k(0, 0, nc.scalar.copy)
-        round_k(0, 1, nc.scalar.copy)
         gather(2, 1)
         nc.vector.tensor_copy(x_bf[:].rearrange("p (c i) t -> p c t i", i=4), x_raw[:].rearrange("p t (c i) -> p c t i", i=4))
         gather(3, 1)
+        round_k(0, 1, nc.vector.tensor_copy)
         turn_k(0, 0, 3)
         turn_k(0, 1, 4)
         make_weight(2)
@@ -208,7 +208,7 @@ def tile_attend_gpq_nce_x_kernel(tc, xT, cb, norm, ts, y, wt, offs, out):
         turn_k(2, 1, 0)
         quantize_k(0, 0)
         quantize(x_codes[:], x_scales[:], x_bf[:].rearrange("p r t -> p (r t)"), E4M3)
-        round_k(1, 1, nc.vector.tensor_copy)
+        round_k(1, 1, nc.scalar.copy)
         quantize_k(0, 1)
         y_banks0 = [turn_y(0, b, 5 + b) for b in range(2)]
         scores(0, 0, 1)
@@ -225,21 +225,19 @@ def tile_attend_gpq_nce_x_kernel(tc, xT, cb, norm, ts, y, wt, offs, out):
         turn_k(3, 1, 6)
         quantize_kt(0, 0)
         quantize_kt(1, 0)
-        for j in range(ROW_TILES):
-            weigh(0, j)
+        weigh(0, slice(0, R))
         for b in range(2):
             residual(1, 1 - b, y_banks1[b])
-        for j in range(ROW_TILES):
-            quantize_h(0, j)
+        quantize_h(0, slice(0, R))
         quantize_kt(0, 1)
         sums = [bank(2 * j, "sums%d" % j) for j in range(ROW_TILES)]
         for j in range(ROW_TILES):
             gradient(0, j, sums[j])
-        weigh(1, 0)
+        weigh(1, slice(0, P))
         quantize_kt(1, 1)
-        quantize_h(1, 0)
-        weigh(1, 1)
-        quantize_h(1, 1)
+        quantize_h(1, slice(0, P))
+        weigh(1, slice(P, R))
+        quantize_h(1, slice(P, R))
         for j in range(ROW_TILES):
             gradient(1, j, sums[j])
             nc.scalar.copy(

@@ -32,47 +32,48 @@ def tile_attend_gpq_nce_x_kernel(tc, xT, cb, norm, ts, y, wt, offs, out):
         sb = ctx.enter_context(tc.tile_pool(name="sb", bufs=1))
         ps = ctx.enter_context(tc.psum_pool(name="ps", bufs=1))
 
-        def bank(index, name):
-            return ps.tile([P, PASS], F32, name=name, tag="bank%d" % index)
+        def bank(index, name, dtype=F32):
+            return ps.tile([P, PASS], dtype, name=name, tag="bank%d" % index)
 
         def tiles(name, count, shape, dtype):
             return [sb.tile(shape, dtype, name="%s%d" % (name, i), align_bytes=64) for i in range(count)]
 
         offsets = sb.tile([P, N // LIST_ROWS], U16, name="offsets")
-        norm_sb = tiles("norm_sb", PASSES, [P, PASS], F32)
-        planes = tiles("planes", PACK, [P, C], F32)
-        x_raw = sb.tile([P, PACK, R], F32, name="x_raw")
-        y_sb = tiles("y_sb", PASSES, [P, ROW_TILES, PASS], F32)
+        norm_sb = sb.tile([P, N], F32, name="norm_sb", align_bytes=64)
+        planes = [sb.tile([P, C], F32, name="plane%d" % t, tag="plane%d" % t, align_bytes=64) for t in range(PACK)]
+        x_raw = sb.tile([P, PACK, R], F32, name="x_raw", tag="x_raw", align_bytes=64)
         ts_col = sb.tile([P, PASSES, PACK], F32, name="ts_col")
-        norm_col = sb.tile([P, PASSES, PACK], F32, name="norm_col")
+        norm_col = sb.tile([P, N // P], F32, name="norm_col")
         wt_col = sb.tile([P, 2], F32, name="wt_col")
 
         cb_planes = cb.rearrange("(p t) c -> t p c", t=PACK)
         y_rows = y.rearrange("(j m) n -> m j n", m=P)
-        nc.sync.dma_start(norm_col[:], norm[0:1, :].rearrange("o (g s t) -> s (o g) t", g=PASSES, t=PACK))
+        nc.sync.dma_start(norm_col[:], norm[0:1, :].rearrange("o (s c) -> s (o c)", s=P))
         nc.sync.dma_start(planes[0][:], cb_planes[0])
         nc.sync.dma_start(offsets[:], offs)
         nc.sync.dma_start(wt_col[:], wt.rearrange("(p e) o -> p (e o)", e=2))
         nc.sync.dma_start(ts_col[:], ts[0:1, :].rearrange("o (g s t) -> s (o g) t", g=PASSES, t=PACK))
-        for t in range(1, PACK):
+        for t in range(1, PACK - 1):
             nc.sync.dma_start(planes[t][:], cb_planes[t])
         nc.sync.dma_start(x_raw[:], xT.rearrange("(p t) r -> p t r", t=PACK))
-        for g in range(PASSES):
-            nc.sync.dma_start(y_sb[g][:], y_rows[:, :, g * PASS : (g + 1) * PASS])
+        nc.sync.dma_start(planes[PACK - 1][:], cb_planes[PACK - 1])
 
         identity = sb.tile([P, P], F32, name="identity")
         make_identity(nc, identity[:])
+        identity_bf = sb.tile([P, P], BF16, name="identity_bf")
+        make_identity(nc, identity_bf[:])
         warm_in = sb.tile([P, 1], F32, name="warm_in")
         warm = sb.tile([P, 1], F32, name="warm")
         nc.vector.memset(warm_in[:], 0.0)
         nc.scalar.activation(warm[:], warm_in[:], SIGMOID)
 
-        for g in range(PASSES):
-            spread = bank(g, "norm_spread")
-            for t in range(PACK):
-                nc.tensor.transpose(spread[:, t * P : (t + 1) * P], norm_col[:, g, t : t + 1].to_broadcast([P, P]), identity[:])
-            nc.scalar.copy(
-                norm_sb[g][:].rearrange("q (s t) -> q s t", t=PACK), spread[:].rearrange("q (t s) -> q s t", t=PACK)
+        for v in range(2):
+            spread = bank(v, "norm_spread")
+            for c in range(4):
+                column = norm_col[:, 4 * v + c : 4 * v + c + 1]
+                nc.tensor.transpose(spread[:, c * P : (c + 1) * P], column.to_broadcast([P, P]), identity[:])
+            (nc.scalar.copy, nc.vector.tensor_copy)[v](
+                norm_sb[:].rearrange("q (s v c) -> q v s c", v=2, c=4)[:, v], spread[:].rearrange("q (c s) -> q s c", c=4)
             )
 
         weight = tiles("weight", PASSES, [P, PACK, R], F32)
@@ -92,11 +93,10 @@ def tile_attend_gpq_nce_x_kernel(tc, xT, cb, norm, ts, y, wt, offs, out):
         k_bf = [tiles("k_bf%d_" % g, 2, [P, 2, P, PACK], BF16) for g in range(PASSES)]
         k_codes = tiles("k_codes", PASSES, [P, PASS], U32)
         k_scales = tiles("k_scales", PASSES, [P, PASS], U8)
-        kt_bf = [tiles("kt_bf%d_" % g, 2, [P, 2, P, PACK], BF16) for g in range(PASSES)]
-        kt_codes = tiles("kt_codes", PASSES, [P, D], U32)
+        kt_early = tiles("kt_early", PASSES, [P, 2, P, PACK], BF16)
+        kt_bf = [[kt_early[g][:]] for g in range(PASSES)]
         kt_scales = tiles("kt_scales", PASSES, [P, D], U8)
         x_bf = sb.tile([P, R, PACK], BF16, name="x_bf", align_bytes=64)
-        x_codes = sb.tile([P, R], U32, name="x_codes", align_bytes=64)
         x_scales = sb.tile([P, R], U8, name="x_scales", align_bytes=64)
         sig = tiles("sig", PASSES, [P, PACK, R], F32)
         diff = tiles("diff", PASSES, [P, PACK, R], F32)
@@ -108,7 +108,7 @@ def tile_attend_gpq_nce_x_kernel(tc, xT, cb, norm, ts, y, wt, offs, out):
         def gather(td, g):
             columns = PASS // LIST_ROWS
             window = planes[td][:].indirect(offsets[:, g * columns : (g + 1) * columns])
-            nc.vector.tensor_tensor(gathered[g][:, td, :], window, norm_sb[g][:], MULT)
+            nc.vector.tensor_tensor(gathered[g][:, td, :], window, norm_sb[:, g * PASS : (g + 1) * PASS], MULT)
 
         def round_k(g, b, copy):
             copy(
@@ -122,12 +122,19 @@ def tile_attend_gpq_nce_x_kernel(tc, xT, cb, norm, ts, y, wt, offs, out):
                 nc.tensor.transpose(turned[:, t * P : (t + 1) * P], gathered[g][:, td, t:PASS:PACK], identity[:])
             nc.scalar.copy(kt_bf[g][td // 2][:, td % 2], turned[:].rearrange("s (t p) -> s p t", t=PACK))
 
+        def turn_last_plane(g, index):
+            td = PACK - 1
+            turned = bank(index, "k_turned_bf", BF16)
+            for t in range(PACK):
+                nc.tensor.transpose(turned[:, t * P : (t + 1) * P], k_bf[g][t // 2][:, t % 2, :, td], identity_bf[:])
+            nc.scalar.copy(kt_bf[g][td // 2][:, td % 2], turned[:].rearrange("s (t p) -> s p t", t=PACK))
+
         def quantize(codes, scales, values, fmt):
             nc.vector.quantize_mx(out=codes.bitcast(fmt), scales=scales, in_=values)
 
         def quantize_kt(g, u):
             half = slice(u * D // 2, (u + 1) * D // 2)
-            quantize(kt_codes[g][:, half], kt_scales[g][:, half], kt_bf[g][u][:].rearrange("s e p t -> s (e p t)"), E4M3)
+            quantize(kt_codes[:, g, half], kt_scales[g][:, half], kt_bf[g][u].rearrange("s e p t -> s (e p t)"), E4M3)
 
         def quantize_k(g, b):
             cols = slice(2 * b * P, 2 * (b + 1) * P)
@@ -183,7 +190,7 @@ def tile_attend_gpq_nce_x_kernel(tc, xT, cb, norm, ts, y, wt, offs, out):
                 out=acc[:],
                 lhsT=h_codes[g][:, j * P : (j + 1) * P].bitcast(E5M2),
                 lhsT_scale=h_scales[g][:, j * P : (j + 1) * P],
-                rhs=kt_codes[g][:].bitcast(E4M3),
+                rhs=kt_codes[:, g, :].bitcast(E4M3),
                 rhs_scale=kt_scales[g][:],
                 start=(g == 0),
                 stop=(g == PASSES - 1),
@@ -192,45 +199,44 @@ def tile_attend_gpq_nce_x_kernel(tc, xT, cb, norm, ts, y, wt, offs, out):
         for td in range(PACK - 2):
             for g in range(PASSES):
                 gather(td, g)
-        gather(2, 0)
-        gather(3, 0)
-        round_k(0, 0, nc.scalar.copy)
-        gather(2, 1)
-        nc.vector.tensor_copy(x_bf[:].rearrange("p (c i) t -> p c t i", i=4), x_raw[:].rearrange("p t (c i) -> p c t i", i=4))
-        gather(3, 1)
-        round_k(0, 1, nc.vector.tensor_copy)
-        turn_k(0, 0, 3)
-        turn_k(0, 1, 4)
+                turn_k(td, g, 3 + td * PASSES + g)
+        y_sb = [sb.tile([P, ROW_TILES, PASS], F32, name="y_sb%d" % g, tag="plane%d" % g, align_bytes=64) for g in range(PASSES)]
+        for g in range(PASSES):
+            nc.sync.dma_start(y_sb[g][:], y_rows[:, :, g * PASS : (g + 1) * PASS])
         make_weight(2)
-        turn_k(1, 0, 5)
-        turn_k(1, 1, 6)
-        turn_k(2, 0, 7)
-        turn_k(2, 1, 0)
-        quantize_k(0, 0)
+        nc.scalar.copy(x_bf[:].rearrange("p (c i) t -> p c t i", i=4), x_raw[:].rearrange("p t (c i) -> p c t i", i=4))
+        kt_late = sb.tile([P, PASSES, 2, P, PACK], BF16, name="kt_late", tag="x_raw", align_bytes=64)
+        for g in range(PASSES):
+            kt_bf[g].append(kt_late[:, g])
+            gather(2, g)
+            turn_k(2, g, g)
+        x_codes = sb.tile([P, R], U32, name="x_codes", tag="plane2", align_bytes=64)
         quantize(x_codes[:], x_scales[:], x_bf[:].rearrange("p r t -> p (r t)"), E4M3)
-        round_k(1, 1, nc.scalar.copy)
-        quantize_k(0, 1)
-        y_banks0 = [turn_y(0, b, 5 + b) for b in range(2)]
-        scores(0, 0, 1)
-        scores(0, 1, 2)
+        gather(3, 0)
+        gather(3, 1)
+        kt_codes = sb.tile([P, PASSES, D], U32, name="kt_codes", tag="plane%d" % (PACK - 1), align_bytes=64)
+        round_k(0, 0, nc.scalar.copy)
+        round_k(0, 1, nc.vector.tensor_copy)
         round_k(1, 0, nc.scalar.copy)
-        quantize_k(1, 1)
-        quantize_k(1, 0)
-        scores(1, 1, 4)
-        scores(1, 0, 3)
-        for b in range(2):
-            residual(0, b, y_banks0[b])
-        y_banks1 = [turn_y(1, 1, 7), turn_y(1, 0, 1)]
-        turn_k(3, 0, 5)
-        turn_k(3, 1, 6)
+        round_k(1, 1, nc.scalar.copy)
+        y_banks0 = [turn_y(0, b, b) for b in range(2)]
+        for g in range(PASSES):
+            for b in range(2):
+                quantize_k(g, b)
+                scores(g, b, 3 + 2 * g + b)
         quantize_kt(0, 0)
         quantize_kt(1, 0)
-        weigh(0, slice(0, R))
         for b in range(2):
-            residual(1, 1 - b, y_banks1[b])
+            residual(0, b, y_banks0[b])
+        y_banks1 = [turn_y(1, b, 3 + b) for b in range(2)]
+        turn_last_plane(0, 7)
+        turn_last_plane(1, 5)
+        weigh(0, slice(0, R))
+        residual(1, 0, y_banks1[0])
         quantize_h(0, slice(0, R))
+        residual(1, 1, y_banks1[1])
         quantize_kt(0, 1)
-        sums = [bank(2 * j, "sums%d" % j) for j in range(ROW_TILES)]
+        sums = [bank(j, "sums%d" % j) for j in range(ROW_TILES)]
         for j in range(ROW_TILES):
             gradient(0, j, sums[j])
         weigh(1, slice(0, P))
@@ -240,7 +246,12 @@ def tile_attend_gpq_nce_x_kernel(tc, xT, cb, norm, ts, y, wt, offs, out):
         quantize_h(1, slice(P, R))
         for j in range(ROW_TILES):
             gradient(1, j, sums[j])
-            nc.scalar.copy(
-                result[j][:].rearrange("m (p d) -> m p d", d=PACK), sums[j][:].rearrange("m (d p) -> m p d", d=PACK)
-            )
-            nc.sync.dma_start(out[j * P : (j + 1) * P, :], result[j][:])
+            pieces = j + 1
+            for i in range(pieces):
+                part = slice(i * P // pieces, (i + 1) * P // pieces)
+                cols = slice(i * D // pieces, (i + 1) * D // pieces)
+                nc.scalar.copy(
+                    result[j][:, cols].rearrange("m (p d) -> m p d", d=PACK),
+                    sums[j][:].rearrange("m (d p) -> m p d", d=PACK)[:, part, :],
+                )
+                nc.sync.dma_start(out[j * P : (j + 1) * P, cols], result[j][:, cols])

@@ -51,17 +51,15 @@ def tile_attend_gpq_nce_x_kernel(tc, xT, cb, norm, ts, y, wt, offs, out):
         nc.sync.dma_start(norm_col[:], norm[0:1, :].rearrange("o (s c) -> s (o c)", s=P))
         nc.sync.dma_start(planes[0][:], cb_planes[0])
         nc.sync.dma_start(offsets[:], offs)
-        nc.sync.dma_start(wt_col[:], wt.rearrange("(p e) o -> p (e o)", e=2))
-        nc.sync.dma_start(ts_col[:], ts[0:1, :].rearrange("o (g s t) -> s (o g) t", g=PASSES, t=PACK))
+        nc.scalar.dma_start(wt_col[:], wt.rearrange("(p e) o -> p (e o)", e=2))
+        nc.scalar.dma_start(ts_col[:], ts[0:1, :].rearrange("o (g s t) -> s (o g) t", g=PASSES, t=PACK))
         for t in range(1, PACK - 1):
             nc.sync.dma_start(planes[t][:], cb_planes[t])
-        nc.sync.dma_start(x_raw[:], xT.rearrange("(p t) r -> p t r", t=PACK))
         nc.sync.dma_start(planes[PACK - 1][:], cb_planes[PACK - 1])
+        nc.sync.dma_start(x_raw[:], xT.rearrange("(p t) r -> p t r", t=PACK))
 
         identity = sb.tile([P, P], F32, name="identity")
         make_identity(nc, identity[:])
-        identity_bf = sb.tile([P, P], BF16, name="identity_bf")
-        make_identity(nc, identity_bf[:])
         warm_in = sb.tile([P, 1], F32, name="warm_in")
         warm = sb.tile([P, 1], F32, name="warm")
         nc.vector.memset(warm_in[:], 0.0)
@@ -89,16 +87,19 @@ def tile_attend_gpq_nce_x_kernel(tc, xT, cb, norm, ts, y, wt, offs, out):
                         weight[g][:, t, :].rearrange("q (k e) -> q k e", e=2), wt_row, COPY, scale=ts_col[:, g, t : t + 1]
                     )
 
-        gathered = tiles("gathered", PASSES, [P, PACK, PASS], F32)
-        k_bf = [tiles("k_bf%d_" % g, 2, [P, 2, P, PACK], BF16) for g in range(PASSES)]
-        k_codes = tiles("k_codes", PASSES, [P, PASS], U32)
+        def reuse(tag, name, shape, dtype):
+            return sb.tile(shape, dtype, name=name, tag=tag, align_bytes=64)
+
+        gathered = [reuse("gathered%d" % g, "gathered%d" % g, [P, PACK, PASS], F32) for g in range(PASSES)]
+        k_bf = {}
+        k_codes = {}
         k_scales = tiles("k_scales", PASSES, [P, PASS], U8)
-        kt_early = tiles("kt_early", PASSES, [P, 2, P, PACK], BF16)
-        kt_bf = [[kt_early[g][:]] for g in range(PASSES)]
+        kt_bf = {key: reuse("kt_bf%d%d" % key, "kt_bf%d%d" % key, [P, 2, P, PACK], BF16) for key in ((0, 0), (0, 1), (1, 0), (1, 1))}
         kt_scales = tiles("kt_scales", PASSES, [P, D], U8)
-        x_bf = sb.tile([P, R, PACK], BF16, name="x_bf", align_bytes=64)
+        x_bf = reuse("x_bf", "x_bf", [P, R, PACK], BF16)
+        x_codes = sb.tile([P, R], U32, name="x_codes", align_bytes=64)
         x_scales = sb.tile([P, R], U8, name="x_scales", align_bytes=64)
-        sig = tiles("sig", PASSES, [P, PACK, R], F32)
+        sig = [reuse("sig%d" % g, "sig%d" % g, [P, PACK, R], F32) for g in range(PASSES)]
         diff = tiles("diff", PASSES, [P, PACK, R], F32)
         h_bf = tiles("h_bf", PASSES, [P, R, PACK], BF16)
         h_codes = tiles("h_codes", PASSES, [P, R], U32)
@@ -110,35 +111,38 @@ def tile_attend_gpq_nce_x_kernel(tc, xT, cb, norm, ts, y, wt, offs, out):
             window = planes[td][:].indirect(offsets[:, g * columns : (g + 1) * columns])
             nc.vector.tensor_tensor(gathered[g][:, td, :], window, norm_sb[:, g * PASS : (g + 1) * PASS], MULT)
 
-        def round_k(g, b, copy):
+        def round_k(g, b, copy, rounded):
+            k_bf[g, b] = rounded
             copy(
-                k_bf[g][b][:].rearrange("p t s d -> p s d t"),
+                k_bf[g, b].rearrange("p t s d -> p s d t"),
                 gathered[g][:].rearrange("p d (s t) -> p s d t", t=PACK)[:, :, :, 2 * b : 2 * b + 2],
             )
 
-        def turn_k(td, g, index):
+        def turn_early(td, g, index):
             turned = bank(index, "k_turned")
             for t in range(PACK):
                 nc.tensor.transpose(turned[:, t * P : (t + 1) * P], gathered[g][:, td, t:PASS:PACK], identity[:])
-            nc.scalar.copy(kt_bf[g][td // 2][:, td % 2], turned[:].rearrange("s (t p) -> s p t", t=PACK))
+            nc.scalar.copy(kt_bf[g, td // 2][:, td % 2], turned[:].rearrange("s (t p) -> s p t", t=PACK))
 
-        def turn_last_plane(g, index):
-            td = PACK - 1
-            turned = bank(index, "k_turned_bf", BF16)
+        def turn_late(g, wanted, index):
+            turned = bank(index, "k_turned")
             for t in range(PACK):
-                nc.tensor.transpose(turned[:, t * P : (t + 1) * P], k_bf[g][t // 2][:, t % 2, :, td], identity_bf[:])
-            nc.scalar.copy(kt_bf[g][td // 2][:, td % 2], turned[:].rearrange("s (t p) -> s p t", t=PACK))
+                words = k_bf[g, t // 2].rearrange("p t s d -> p t (s d)").bitcast(F32)
+                nc.tensor.transpose(turned[:, t * P : (t + 1) * P], words[:, t % 2, 1 : 2 * P : 2], identity[:])
+            pairs = turned[:].bitcast(BF16).rearrange("s (t p e) -> s e p t", t=PACK, e=2)
+            for e in wanted:
+                nc.scalar.copy(kt_bf[g, 1][:, e], pairs[:, e])
 
         def quantize(codes, scales, values, fmt):
             nc.vector.quantize_mx(out=codes.bitcast(fmt), scales=scales, in_=values)
 
         def quantize_kt(g, u):
             half = slice(u * D // 2, (u + 1) * D // 2)
-            quantize(kt_codes[:, g, half], kt_scales[g][:, half], kt_bf[g][u].rearrange("s e p t -> s (e p t)"), E4M3)
+            quantize(kt_codes[:, g, half], kt_scales[g][:, half], kt_bf[g, u][:].rearrange("s e p t -> s (e p t)"), E4M3)
 
         def quantize_k(g, b):
             cols = slice(2 * b * P, 2 * (b + 1) * P)
-            quantize(k_codes[g][:, cols], k_scales[g][:, cols], k_bf[g][b][:].rearrange("p t s d -> p (t s d)"), E4M3)
+            quantize(k_codes[g, b], k_scales[g][:, cols], k_bf[g, b].rearrange("p t s d -> p (t s d)"), E4M3)
 
         def turn_y(g, b, index):
             turned = bank(index, "y_turned")
@@ -154,7 +158,7 @@ def tile_attend_gpq_nce_x_kernel(tc, xT, cb, norm, ts, y, wt, offs, out):
                 cols = slice(t * P, (t + 1) * P)
                 nc.tensor.matmul_mx(
                     out=acc[:, (t % 2) * R : (t % 2 + 1) * R],
-                    lhsT=k_codes[g][:, cols].bitcast(E4M3),
+                    lhsT=k_codes[g, b][:, (t % 2) * P : (t % 2 + 1) * P].bitcast(E4M3),
                     lhsT_scale=k_scales[g][:, cols],
                     rhs=x_codes[:].bitcast(E4M3),
                     rhs_scale=x_scales[:],
@@ -199,44 +203,50 @@ def tile_attend_gpq_nce_x_kernel(tc, xT, cb, norm, ts, y, wt, offs, out):
         for td in range(PACK - 2):
             for g in range(PASSES):
                 gather(td, g)
-                turn_k(td, g, 3 + td * PASSES + g)
-        y_sb = [sb.tile([P, ROW_TILES, PASS], F32, name="y_sb%d" % g, tag="plane%d" % g, align_bytes=64) for g in range(PASSES)]
+                turn_early(td, g, 3 + td * PASSES + g)
+        y_sb = [reuse("plane%d" % g, "y_sb%d" % g, [P, ROW_TILES, PASS], F32) for g in range(PASSES)]
         for g in range(PASSES):
             nc.sync.dma_start(y_sb[g][:], y_rows[:, :, g * PASS : (g + 1) * PASS])
         make_weight(2)
-        nc.scalar.copy(x_bf[:].rearrange("p (c i) t -> p c t i", i=4), x_raw[:].rearrange("p t (c i) -> p c t i", i=4))
-        kt_late = sb.tile([P, PASSES, 2, P, PACK], BF16, name="kt_late", tag="x_raw", align_bytes=64)
-        for g in range(PASSES):
-            kt_bf[g].append(kt_late[:, g])
-            gather(2, g)
-            turn_k(2, g, g)
-        x_codes = sb.tile([P, R], U32, name="x_codes", tag="plane2", align_bytes=64)
-        quantize(x_codes[:], x_scales[:], x_bf[:].rearrange("p r t -> p (r t)"), E4M3)
+        gather(2, 0)
+        turn_early(2, 0, 7)
+        gather(2, 1)
         gather(3, 0)
         gather(3, 1)
-        kt_codes = sb.tile([P, PASSES, D], U32, name="kt_codes", tag="plane%d" % (PACK - 1), align_bytes=64)
-        round_k(0, 0, nc.scalar.copy)
-        round_k(0, 1, nc.vector.tensor_copy)
-        round_k(1, 0, nc.scalar.copy)
-        round_k(1, 1, nc.scalar.copy)
+        nc.scalar.copy(x_bf[:].rearrange("p (c i) t -> p c t i", i=4), x_raw[:].rearrange("p t (c i) -> p c t i", i=4))
+        round_k(0, 0, nc.vector.tensor_copy, reuse("k_bf00", "k_bf00", [P, 2, P, PACK], BF16)[:])
+        after_x = reuse("x_raw", "k_bf_after_x", [P, 3, 2, P, PACK], BF16)
+        round_k(0, 1, nc.scalar.copy, after_x[:, 0])
+        round_k(1, 0, nc.scalar.copy, after_x[:, 1])
+        quantize(x_codes[:], x_scales[:], x_bf[:].rearrange("p r t -> p (r t)"), E4M3)
+        first_codes = reuse("x_bf", "k_codes0", [P, 2, 2 * P], U32)
+        k_codes[0, 0] = first_codes[:, 0, :]
+        k_codes[0, 1] = first_codes[:, 1, :]
+        k_codes[1, 0] = reuse("k_codes10", "k_codes10", [P, 2 * P], U32)[:]
+        kt_codes = reuse("gathered0", "kt_codes", [P, PASSES, D], U32)
         y_banks0 = [turn_y(0, b, b) for b in range(2)]
-        for g in range(PASSES):
-            for b in range(2):
-                quantize_k(g, b)
-                scores(g, b, 3 + 2 * g + b)
+        for b in range(2):
+            quantize_k(0, b)
+            scores(0, b, 5 + b)
+        round_k(1, 1, nc.vector.tensor_copy, after_x[:, 2])
+        quantize_k(1, 0)
+        scores(1, 0, 7)
+        k_codes[1, 1] = reuse("k_codes11", "k_codes11", [P, 2 * P], U32)[:]
+        quantize_k(1, 1)
+        scores(1, 1, 2)
         quantize_kt(0, 0)
         quantize_kt(1, 0)
         for b in range(2):
             residual(0, b, y_banks0[b])
-        y_banks1 = [turn_y(1, b, 3 + b) for b in range(2)]
-        turn_last_plane(0, 7)
-        turn_last_plane(1, 5)
+        y_banks1 = [turn_y(1, b, 6 + b) for b in range(2)]
+        turn_late(0, (1,), 0)
+        turn_late(1, (0, 1), 2)
         weigh(0, slice(0, R))
         residual(1, 0, y_banks1[0])
         quantize_h(0, slice(0, R))
         residual(1, 1, y_banks1[1])
         quantize_kt(0, 1)
-        sums = [bank(j, "sums%d" % j) for j in range(ROW_TILES)]
+        sums = [bank(index, "sums") for index in (3, 4)]
         for j in range(ROW_TILES):
             gradient(0, j, sums[j])
         weigh(1, slice(0, P))
@@ -250,7 +260,7 @@ def tile_attend_gpq_nce_x_kernel(tc, xT, cb, norm, ts, y, wt, offs, out):
             for i in range(pieces):
                 part = slice(i * P // pieces, (i + 1) * P // pieces)
                 cols = slice(i * D // pieces, (i + 1) * D // pieces)
-                nc.scalar.copy(
+                (nc.scalar.copy, nc.vector.tensor_copy)[j](
                     result[j][:, cols].rearrange("m (p d) -> m p d", d=PACK),
                     sums[j][:].rearrange("m (d p) -> m p d", d=PACK)[:, part, :],
                 )

@@ -60,10 +60,6 @@ def tile_attend_gpq_nce_x_kernel(tc, xT, cb, norm, ts, y, wt, offs, out):
 
         identity = sb.tile([P, P], F32, name="identity")
         make_identity(nc, identity[:])
-        warm_in = sb.tile([P, 1], F32, name="warm_in")
-        warm = sb.tile([P, 1], F32, name="warm")
-        nc.vector.memset(warm_in[:], 0.0)
-        nc.scalar.activation(warm[:], warm_in[:], SIGMOID)
 
         for v in range(2):
             spread = bank(v, "norm_spread")

@@ -39,35 +39,35 @@ def tile_attend_gpq_nce_x_kernel(tc, xT, cb, norm, ts, y, wt, offs, out):
             return [sb.tile(shape, dtype, name="%s%d" % (name, i), align_bytes=64) for i in range(count)]
 
         offsets = sb.tile([P, N // LIST_ROWS], U16, name="offsets")
-        norm_sb = sb.tile([P, N], F32, name="norm_sb", align_bytes=64)
+        norm_sb = sb.tile([P, N], F32, name="norm_sb", tag="norm_sb", align_bytes=64)
         planes = [sb.tile([P, C], F32, name="plane%d" % t, tag="plane%d" % t, align_bytes=64) for t in range(PACK)]
-        x_raw = sb.tile([P, PACK, R], F32, name="x_raw", tag="x_raw", align_bytes=64)
         ts_col = sb.tile([P, PASSES, PACK], F32, name="ts_col")
-        norm_col = sb.tile([P, N // P], F32, name="norm_col")
+        norm_col = sb.tile([P, PASSES, PACK], F32, name="norm_col")
         wt_col = sb.tile([P, 2], F32, name="wt_col")
 
         cb_planes = cb.rearrange("(p t) c -> t p c", t=PACK)
         y_rows = y.rearrange("(j m) n -> m j n", m=P)
-        nc.sync.dma_start(norm_col[:], norm[0:1, :].rearrange("o (s c) -> s (o c)", s=P))
+        nc.sync.dma_start(norm_col[:], norm[0:1, :].rearrange("o (g s t) -> s (o g) t", g=PASSES, t=PACK))
         nc.sync.dma_start(planes[0][:], cb_planes[0])
         nc.sync.dma_start(offsets[:], offs)
-        nc.scalar.dma_start(wt_col[:], wt.rearrange("(p e) o -> p (e o)", e=2))
-        nc.scalar.dma_start(ts_col[:], ts[0:1, :].rearrange("o (g s t) -> s (o g) t", g=PASSES, t=PACK))
+        nc.sync.dma_start(wt_col[:], wt.rearrange("(p e) o -> p (e o)", e=2))
+        nc.sync.dma_start(ts_col[:], ts[0:1, :].rearrange("o (g s t) -> s (o g) t", g=PASSES, t=PACK))
         for t in range(1, PACK - 1):
             nc.sync.dma_start(planes[t][:], cb_planes[t])
         nc.sync.dma_start(planes[PACK - 1][:], cb_planes[PACK - 1])
-        nc.sync.dma_start(x_raw[:], xT.rearrange("(p t) r -> p t r", t=PACK))
 
         identity = sb.tile([P, P], F32, name="identity")
         make_identity(nc, identity[:])
+        warm = sb.tile([P, 1], F32, name="warm")
+        nc.scalar.activation(warm[:], identity[:, 0:1], SIGMOID)
 
-        for v in range(2):
-            spread = bank(v, "norm_spread")
-            for c in range(4):
-                column = norm_col[:, 4 * v + c : 4 * v + c + 1]
-                nc.tensor.transpose(spread[:, c * P : (c + 1) * P], column.to_broadcast([P, P]), identity[:])
-            (nc.scalar.copy, nc.vector.tensor_copy)[v](
-                norm_sb[:].rearrange("q (s v c) -> q v s c", v=2, c=4)[:, v], spread[:].rearrange("q (c s) -> q s c", c=4)
+        for g in range(PASSES):
+            spread = bank(g, "norm_spread")
+            for t in range(PACK):
+                nc.tensor.transpose(spread[:, t * P : (t + 1) * P], norm_col[:, g, t : t + 1].to_broadcast([P, P]), identity[:])
+            nc.scalar.copy(
+                norm_sb[:, g * PASS : (g + 1) * PASS].rearrange("q (s t) -> q s t", t=PACK),
+                spread[:].rearrange("q (t s) -> q s t", t=PACK),
             )
 
         weight = tiles("weight", PASSES, [P, PACK, R], F32)
@@ -86,13 +86,13 @@ def tile_attend_gpq_nce_x_kernel(tc, xT, cb, norm, ts, y, wt, offs, out):
         def reuse(tag, name, shape, dtype):
             return sb.tile(shape, dtype, name=name, tag=tag, align_bytes=64)
 
-        gathered = [reuse("gathered%d" % g, "gathered%d" % g, [P, PACK, PASS], F32) for g in range(PASSES)]
+        columns_k = sb.tile([P, PACK, N], F32, name="columns_k", align_bytes=64)
+        gathered = [columns_k[:, :, g * PASS : (g + 1) * PASS] for g in range(PASSES)]
         k_bf = {}
         k_codes = {}
         k_scales = tiles("k_scales", PASSES, [P, PASS], U8)
         kt_bf = {key: reuse("kt_bf%d%d" % key, "kt_bf%d%d" % key, [P, 2, P, PACK], BF16) for key in ((0, 0), (0, 1), (1, 0), (1, 1))}
         kt_scales = tiles("kt_scales", PASSES, [P, D], U8)
-        x_bf = reuse("x_bf", "x_bf", [P, R, PACK], BF16)
         x_codes = sb.tile([P, R], U32, name="x_codes", align_bytes=64)
         x_scales = sb.tile([P, R], U8, name="x_scales", align_bytes=64)
         sig = [reuse("sig%d" % g, "sig%d" % g, [P, PACK, R], F32) for g in range(PASSES)]
@@ -111,7 +111,7 @@ def tile_attend_gpq_nce_x_kernel(tc, xT, cb, norm, ts, y, wt, offs, out):
             k_bf[g, b] = rounded
             copy(
                 k_bf[g, b].rearrange("p t s d -> p s d t"),
-                gathered[g][:].rearrange("p d (s t) -> p s d t", t=PACK)[:, :, :, 2 * b : 2 * b + 2],
+                gathered[g].rearrange("p d (s t) -> p s d t", t=PACK)[:, :, :, 2 * b : 2 * b + 2],
             )
 
         def turn_early(td, g, index):
@@ -176,9 +176,9 @@ def tile_attend_gpq_nce_x_kernel(tc, xT, cb, norm, ts, y, wt, offs, out):
 
         def weigh(g, rows):
             nc.vector.tensor_tensor(
-                h_bf[g][:, rows, :].rearrange("s (c i) t -> s c t i", i=4),
-                diff[g][:, :, rows].rearrange("s t (c i) -> s c t i", i=4),
-                weight[g][:, :, rows].rearrange("s t (c i) -> s c t i", i=4),
+                h_bf[g][:, rows, :].rearrange("s (c i) t -> s c t i", i=2),
+                diff[g][:, :, rows].rearrange("s t (c i) -> s c t i", i=2),
+                weight[g][:, :, rows].rearrange("s t (c i) -> s c t i", i=2),
                 MULT,
             )
 
@@ -196,53 +196,60 @@ def tile_attend_gpq_nce_x_kernel(tc, xT, cb, norm, ts, y, wt, offs, out):
                 stop=(g == PASSES - 1),
             )
 
-        for td in range(PACK - 2):
-            for g in range(PASSES):
-                gather(td, g)
-                turn_early(td, g, 3 + td * PASSES + g)
-        y_sb = [reuse("plane%d" % g, "y_sb%d" % g, [P, ROW_TILES, PASS], F32) for g in range(PASSES)]
-        for g in range(PASSES):
+        y_sb = {}
+
+        def load_y(g, tag):
+            y_sb[g] = reuse(tag, "y_sb%d" % g, [P, ROW_TILES, PASS], F32)
             nc.sync.dma_start(y_sb[g][:], y_rows[:, :, g * PASS : (g + 1) * PASS])
-        make_weight(2)
-        gather(2, 0)
+
+        def gather_whole(td):
+            nc.vector.tensor_tensor(columns_k[:, td, :], planes[td][:].indirect(offsets[:]), norm_sb[:], MULT)
+
+        for td in range(2):
+            gather_whole(td)
+            for g in range(PASSES):
+                turn_early(td, g, 3 + td * PASSES + g)
+        load_y(0, "plane0")
+        x_raw = reuse("plane1", "x_raw", [P, PACK, R], F32)
+        nc.sync.dma_start(x_raw[:], xT.rearrange("(p t) r -> p t r", t=PACK))
+        make_weight(1)
+        gather_whole(2)
         turn_early(2, 0, 7)
-        gather(2, 1)
+        load_y(1, "plane2")
         gather(3, 0)
         gather(3, 1)
-        nc.scalar.copy(x_bf[:].rearrange("p (c i) t -> p c t i", i=4), x_raw[:].rearrange("p t (c i) -> p c t i", i=4))
-        round_k(0, 0, nc.vector.tensor_copy, reuse("k_bf00", "k_bf00", [P, 2, P, PACK], BF16)[:])
-        after_x = reuse("x_raw", "k_bf_after_x", [P, 3, 2, P, PACK], BF16)
-        round_k(0, 1, nc.scalar.copy, after_x[:, 0])
-        round_k(1, 0, nc.scalar.copy, after_x[:, 1])
+        rounded = {key: reuse("k_bf%d%d" % key, "k_bf%d%d" % key, [P, 2, P, PACK], BF16) for key in ((0, 0), (0, 1), (1, 1))}
+        for key in ((0, 0), (1, 0)):
+            k_codes[key] = reuse("k_codes%d%d" % key, "k_codes%d%d" % key, [P, 2 * P], U32)[:]
+        x_bf = reuse("norm_sb", "x_bf", [P, R, PACK], BF16)
+        round_k(0, 0, nc.scalar.copy, rounded[0, 0][:])
+        round_k(0, 1, nc.scalar.copy, rounded[0, 1][:])
+        nc.vector.tensor_copy(x_bf[:].rearrange("p (c i) t -> p c t i", i=2), x_raw[:].rearrange("p t (c i) -> p c t i", i=2))
+        round_k(1, 1, nc.scalar.copy, rounded[1, 1][:])
         quantize(x_codes[:], x_scales[:], x_bf[:].rearrange("p r t -> p (r t)"), E4M3)
-        first_codes = reuse("x_bf", "k_codes0", [P, 2, 2 * P], U32)
-        k_codes[0, 0] = first_codes[:, 0, :]
-        k_codes[0, 1] = first_codes[:, 1, :]
-        k_codes[1, 0] = reuse("k_codes10", "k_codes10", [P, 2 * P], U32)[:]
-        kt_codes = reuse("gathered0", "kt_codes", [P, PASSES, D], U32)
+        round_k(1, 0, nc.vector.tensor_copy, reuse("norm_sb", "k_bf10", [P, 2, P, PACK], BF16)[:])
+        after_x = reuse("plane1", "after_x", [P, PASSES + 1, D], U32)
+        kt_codes = after_x[:, 0:PASSES, :]
+        for g in range(PASSES):
+            k_codes[g, 1] = after_x[:, PASSES, g * 2 * P : (g + 1) * 2 * P]
         y_banks0 = [turn_y(0, b, b) for b in range(2)]
-        for b in range(2):
-            quantize_k(0, b)
-            scores(0, b, 5 + b)
-        round_k(1, 1, nc.vector.tensor_copy, after_x[:, 2])
-        quantize_k(1, 0)
-        scores(1, 0, 7)
-        k_codes[1, 1] = reuse("k_codes11", "k_codes11", [P, 2 * P], U32)[:]
-        quantize_k(1, 1)
-        scores(1, 1, 2)
+        y_banks1 = [turn_y(1, b, 6 + b) for b in range(2)]
+        for g in range(PASSES):
+            for b in range(2):
+                quantize_k(g, b)
+                scores(g, b, 2 + 2 * g + b)
         quantize_kt(0, 0)
         quantize_kt(1, 0)
         for b in range(2):
             residual(0, b, y_banks0[b])
-        y_banks1 = [turn_y(1, b, 6 + b) for b in range(2)]
-        turn_late(0, (1,), 0)
-        turn_late(1, (0, 1), 2)
+        turn_late(0, (1,), 2)
+        turn_late(1, (0, 1), 3)
         weigh(0, slice(0, R))
         residual(1, 0, y_banks1[0])
         quantize_h(0, slice(0, R))
         residual(1, 1, y_banks1[1])
         quantize_kt(0, 1)
-        sums = [bank(index, "sums") for index in (3, 4)]
+        sums = [bank(index, "sums") for index in (0, 1)]
         for j in range(ROW_TILES):
             gradient(0, j, sums[j])
         weigh(1, slice(0, P))

@@ -41,17 +41,17 @@ def tile_attend_gpq_nce_x_kernel(tc, xT, cb, norm, ts, y, wt, offs, out):
         offsets = sb.tile([P, N // LIST_ROWS], U16, name="offsets")
         norm_sb = sb.tile([P, N], F32, name="norm_sb", tag="norm_sb", align_bytes=64)
         planes = [sb.tile([P, C], F32, name="plane%d" % t, tag="plane%d" % t, align_bytes=64) for t in range(PACK)]
-        ts_col = sb.tile([P, PASSES, PACK], F32, name="ts_col")
-        norm_col = sb.tile([P, PASSES, PACK], F32, name="norm_col")
+        ts_col = sb.tile([P, PASSES, 2 * PACK], F32, name="ts_col")
+        norm_col = sb.tile([P, N // P], F32, name="norm_col")
         wt_col = sb.tile([P, 2], F32, name="wt_col")
 
         cb_planes = cb.rearrange("(p t) c -> t p c", t=PACK)
         y_rows = y.rearrange("(j m) n -> m j n", m=P)
-        nc.sync.dma_start(norm_col[:], norm[0:1, :].rearrange("o (g s t) -> s (o g) t", g=PASSES, t=PACK))
+        nc.sync.dma_start(norm_col[:], norm[0:1, :].rearrange("o (s c) -> s (o c)", s=P))
         nc.sync.dma_start(planes[0][:], cb_planes[0])
         nc.sync.dma_start(offsets[:], offs)
-        nc.sync.dma_start(wt_col[:], wt.rearrange("(p e) o -> p (e o)", e=2))
-        nc.sync.dma_start(ts_col[:], ts[0:1, :].rearrange("o (g s t) -> s (o g) t", g=PASSES, t=PACK))
+        nc.scalar.dma_start(wt_col[:], wt.rearrange("(p e) o -> p (e o)", e=2))
+        nc.scalar.dma_start(ts_col[:, :, 0:PACK], ts[0:1, :].rearrange("o (g s t) -> s (o g) t", g=PASSES, t=PACK))
         for t in range(1, PACK - 1):
             nc.sync.dma_start(planes[t][:], cb_planes[t])
         nc.sync.dma_start(planes[PACK - 1][:], cb_planes[PACK - 1])
@@ -61,13 +61,13 @@ def tile_attend_gpq_nce_x_kernel(tc, xT, cb, norm, ts, y, wt, offs, out):
         warm = sb.tile([P, 1], F32, name="warm")
         nc.scalar.activation(warm[:], identity[:, 0:1], SIGMOID)
 
-        for g in range(PASSES):
-            spread = bank(g, "norm_spread")
-            for t in range(PACK):
-                nc.tensor.transpose(spread[:, t * P : (t + 1) * P], norm_col[:, g, t : t + 1].to_broadcast([P, P]), identity[:])
+        for v in range(2):
+            spread = bank(v, "norm_spread")
+            for c in range(4):
+                column = norm_col[:, 4 * v + c : 4 * v + c + 1]
+                nc.tensor.transpose(spread[:, c * P : (c + 1) * P], column.to_broadcast([P, P]), identity[:])
             nc.scalar.copy(
-                norm_sb[:, g * PASS : (g + 1) * PASS].rearrange("q (s t) -> q s t", t=PACK),
-                spread[:].rearrange("q (t s) -> q s t", t=PACK),
+                norm_sb[:].rearrange("q (s v c) -> q v s c", v=2, c=4)[:, v], spread[:].rearrange("q (c s) -> q s c", c=4)
             )
 
         weight = tiles("weight", PASSES, [P, PACK, R], F32)
@@ -219,8 +219,7 @@ def tile_attend_gpq_nce_x_kernel(tc, xT, cb, norm, ts, y, wt, offs, out):
         gather(3, 0)
         gather(3, 1)
         rounded = {key: reuse("k_bf%d%d" % key, "k_bf%d%d" % key, [P, 2, P, PACK], BF16) for key in ((0, 0), (0, 1), (1, 1))}
-        for key in ((0, 0), (1, 0)):
-            k_codes[key] = reuse("k_codes%d%d" % key, "k_codes%d%d" % key, [P, 2 * P], U32)[:]
+        k_codes[0, 0] = reuse("k_codes00", "k_codes00", [P, 2 * P], U32)[:]
         x_bf = reuse("norm_sb", "x_bf", [P, R, PACK], BF16)
         round_k(0, 0, nc.scalar.copy, rounded[0, 0][:])
         round_k(0, 1, nc.scalar.copy, rounded[0, 1][:])
@@ -228,10 +227,11 @@ def tile_attend_gpq_nce_x_kernel(tc, xT, cb, norm, ts, y, wt, offs, out):
         round_k(1, 1, nc.scalar.copy, rounded[1, 1][:])
         quantize(x_codes[:], x_scales[:], x_bf[:].rearrange("p r t -> p (r t)"), E4M3)
         round_k(1, 0, nc.vector.tensor_copy, reuse("norm_sb", "k_bf10", [P, 2, P, PACK], BF16)[:])
-        after_x = reuse("plane1", "after_x", [P, PASSES + 1, D], U32)
+        after_x = reuse("plane1", "after_x", [P, 2 * PASSES, D], U32)
         kt_codes = after_x[:, 0:PASSES, :]
-        for g in range(PASSES):
-            k_codes[g, 1] = after_x[:, PASSES, g * 2 * P : (g + 1) * 2 * P]
+        k_codes[0, 1] = after_x[:, PASSES, 0 : 2 * P]
+        for b in range(2):
+            k_codes[1, b] = after_x[:, PASSES + 1, b * 2 * P : (b + 1) * 2 * P]
         y_banks0 = [turn_y(0, b, b) for b in range(2)]
         y_banks1 = [turn_y(1, b, 6 + b) for b in range(2)]
         for g in range(PASSES):
@@ -259,7 +259,7 @@ def tile_attend_gpq_nce_x_kernel(tc, xT, cb, norm, ts, y, wt, offs, out):
         quantize_h(1, slice(P, R))
         for j in range(ROW_TILES):
             gradient(1, j, sums[j])
-            pieces = j + 1
+            pieces = 2
             for i in range(pieces):
                 part = slice(i * P // pieces, (i + 1) * P // pieces)
                 cols = slice(i * D // pieces, (i + 1) * D // pieces)

@@ -30,6 +30,7 @@ def tile_attend_gpq_nce_x_kernel(tc, xT, cb, norm, ts, y, wt, offs, out):
     nc = tc.nc
     with ExitStack() as ctx:
         sb = ctx.enter_context(tc.tile_pool(name="sb", bufs=1))
+        shared = ctx.enter_context(tc.tile_pool(name="shared", bufs=1))
         ps = ctx.enter_context(tc.psum_pool(name="ps", bufs=1))
 
         def bank(index, name, dtype=F32):
@@ -38,50 +39,62 @@ def tile_attend_gpq_nce_x_kernel(tc, xT, cb, norm, ts, y, wt, offs, out):
         def tiles(name, count, shape, dtype):
             return [sb.tile(shape, dtype, name="%s%d" % (name, i), align_bytes=64) for i in range(count)]
 
+        def placed(name, plane, column, shape, dtype):
+            return shared.tile(shape, dtype, name=name, align_bytes=64, offset=4 * (plane * C + column))
+
         offsets = sb.tile([P, N // LIST_ROWS], U16, name="offsets")
         norm_sb = sb.tile([P, N], F32, name="norm_sb", tag="norm_sb", align_bytes=64)
-        planes = [sb.tile([P, C], F32, name="plane%d" % t, tag="plane%d" % t, align_bytes=64) for t in range(PACK)]
+        planes = [placed("plane%d" % t, t, 0, [P, C], F32) for t in range(PACK - 1)]
         ts_col = sb.tile([P, PASSES, 2 * PACK], F32, name="ts_col")
-        norm_col = sb.tile([P, N // P], F32, name="norm_col")
-        wt_col = sb.tile([P, 2], F32, name="wt_col")
+        norm_col = placed("norm_col", PACK - 1, 0, [P, N // P], F32)
+        wt_col = sb.tile([P, 2], F32, name="wt_col", tag="raw", align_bytes=64)
 
         cb_planes = cb.rearrange("(p t) c -> t p c", t=PACK)
         y_rows = y.rearrange("(j m) n -> m j n", m=P)
+        nc.sync.dma_start(wt_col[:], wt.rearrange("(p e) o -> p (e o)", e=2))
+        nc.sync.dma_start(ts_col[:, :, 0:PACK], ts[0:1, :].rearrange("o (g s t) -> s (o g) t", g=PASSES, t=PACK))
         nc.sync.dma_start(norm_col[:], norm[0:1, :].rearrange("o (s c) -> s (o c)", s=P))
         nc.sync.dma_start(planes[0][:], cb_planes[0])
         nc.sync.dma_start(offsets[:], offs)
-        nc.scalar.dma_start(wt_col[:], wt.rearrange("(p e) o -> p (e o)", e=2))
-        nc.scalar.dma_start(ts_col[:, :, 0:PACK], ts[0:1, :].rearrange("o (g s t) -> s (o g) t", g=PASSES, t=PACK))
         for t in range(1, PACK - 1):
             nc.sync.dma_start(planes[t][:], cb_planes[t])
-        nc.sync.dma_start(planes[PACK - 1][:], cb_planes[PACK - 1])
 
         identity = sb.tile([P, P], F32, name="identity")
         make_identity(nc, identity[:])
         warm = sb.tile([P, 1], F32, name="warm")
         nc.scalar.activation(warm[:], identity[:, 0:1], SIGMOID)
 
-        for v in range(2):
-            spread = bank(v, "norm_spread")
-            for c in range(4):
-                column = norm_col[:, 4 * v + c : 4 * v + c + 1]
-                nc.tensor.transpose(spread[:, c * P : (c + 1) * P], column.to_broadcast([P, P]), identity[:])
-            nc.scalar.copy(
-                norm_sb[:].rearrange("q (s v c) -> q v s c", v=2, c=4)[:, v], spread[:].rearrange("q (c s) -> q s c", c=4)
+        def spread(index, name, columns):
+            turned = bank(index, name)
+            for c, column in enumerate(columns):
+                nc.tensor.transpose(turned[:, c * P : (c + 1) * P], column.to_broadcast([P, P]), identity[:])
+            return turned
+
+        wt_columns = [wt_col[:, e : e + 1] for e in range(2)]
+        weight = tiles("weight", PASSES, [P, PACK, R], F32)
+        wt_bank = spread(2, "wt_bank", wt_columns)
+        nc.vector.tensor_tensor(
+            weight[0][:].rearrange("s t (k e) -> s t k e", e=2),
+            wt_bank[:, 0:R].rearrange("q (e k) -> q k e", e=2).unsqueeze(1).to_broadcast([P, PACK, P, 2]),
+            ts_col[:, 0, 0:PACK].unsqueeze(2).unsqueeze(3).to_broadcast([P, PACK, P, 2]),
+            MULT,
+        )
+        wt_bank = spread(7, "wt_bank", wt_columns)
+        for t in range(PACK):
+            nc.scalar.activation(
+                weight[1][:, t, :].rearrange("q (k e) -> q k e", e=2),
+                wt_bank[:, 0:R].rearrange("q (e k) -> q k e", e=2),
+                COPY,
+                scale=ts_col[:, 1, t : t + 1],
+            )
+        for v, copy in enumerate((nc.vector.tensor_copy, nc.scalar.copy)):
+            norm_bank = spread(v, "norm_bank", [norm_col[:, 4 * v + c : 4 * v + c + 1] for c in range(4)])
+            copy(
+                norm_sb[:].rearrange("q (s v c) -> q v s c", v=2, c=4)[:, v], norm_bank[:].rearrange("q (c s) -> q s c", c=4)
             )
 
-        weight = tiles("weight", PASSES, [P, PACK, R], F32)
-
-        def make_weight(index):
-            wt_bank = bank(index, "wt_bank")
-            for e in range(2):
-                nc.tensor.transpose(wt_bank[:, e * P : (e + 1) * P], wt_col[:, e : e + 1].to_broadcast([P, P]), identity[:])
-            wt_row = wt_bank[:, 0:R].rearrange("q (e k) -> q k e", e=2)
-            for g in range(PASSES):
-                for t in range(PACK):
-                    nc.scalar.activation(
-                        weight[g][:, t, :].rearrange("q (k e) -> q k e", e=2), wt_row, COPY, scale=ts_col[:, g, t : t + 1]
-                    )
+        planes.append(placed("plane3", PACK - 1, 0, [P, C], F32))
+        nc.sync.dma_start(planes[PACK - 1][:], cb_planes[PACK - 1])
 
         def reuse(tag, name, shape, dtype):
             return sb.tile(shape, dtype, name=name, tag=tag, align_bytes=64)
@@ -107,11 +120,20 @@ def tile_attend_gpq_nce_x_kernel(tc, xT, cb, norm, ts, y, wt, offs, out):
             window = planes[td][:].indirect(offsets[:, g * columns : (g + 1) * columns])
             nc.vector.tensor_tensor(gathered[g][:, td, :], window, norm_sb[:, g * PASS : (g + 1) * PASS], MULT)
 
-        def round_k(g, b, copy, rounded):
+        def gather_plain(td, g):
+            columns = PASS // LIST_ROWS
+            raw = reuse("raw", "raw", [P, PASS], F32)
+            nc.scalar.activation(raw[:], planes[td][:].indirect(offsets[:, g * columns : (g + 1) * columns]), COPY)
+            return raw
+
+        def scale(td, g, raw):
+            nc.vector.tensor_tensor(gathered[g][:, td, :], raw[:], norm_sb[:, g * PASS : (g + 1) * PASS], MULT)
+
+        def round_k(g, b, copy, rounded, part=slice(0, P)):
             k_bf[g, b] = rounded
             copy(
-                k_bf[g, b].rearrange("p t s d -> p s d t"),
-                gathered[g].rearrange("p d (s t) -> p s d t", t=PACK)[:, :, :, 2 * b : 2 * b + 2],
+                k_bf[g, b].rearrange("p t s d -> p s d t")[:, part],
+                gathered[g].rearrange("p d (s t) -> p s d t", t=PACK)[:, part, :, 2 * b : 2 * b + 2],
             )
 
         def turn_early(td, g, index):
@@ -134,7 +156,7 @@ def tile_attend_gpq_nce_x_kernel(tc, xT, cb, norm, ts, y, wt, offs, out):
 
         def quantize_kt(g, u):
             half = slice(u * D // 2, (u + 1) * D // 2)
-            quantize(kt_codes[:, g, half], kt_scales[g][:, half], kt_bf[g, u][:].rearrange("s e p t -> s (e p t)"), E4M3)
+            quantize(kt_codes[g][:, half], kt_scales[g][:, half], kt_bf[g, u][:].rearrange("s e p t -> s (e p t)"), E4M3)
 
         def quantize_k(g, b):
             cols = slice(2 * b * P, 2 * (b + 1) * P)
@@ -190,7 +212,7 @@ def tile_attend_gpq_nce_x_kernel(tc, xT, cb, norm, ts, y, wt, offs, out):
                 out=acc[:],
                 lhsT=h_codes[g][:, j * P : (j + 1) * P].bitcast(E5M2),
                 lhsT_scale=h_scales[g][:, j * P : (j + 1) * P],
-                rhs=kt_codes[:, g, :].bitcast(E4M3),
+                rhs=kt_codes[g][:, :].bitcast(E4M3),
                 rhs_scale=kt_scales[g][:],
                 start=(g == 0),
                 stop=(g == PASSES - 1),
@@ -198,56 +220,63 @@ def tile_attend_gpq_nce_x_kernel(tc, xT, cb, norm, ts, y, wt, offs, out):
 
         y_sb = {}
 
-        def load_y(g, tag):
-            y_sb[g] = reuse(tag, "y_sb%d" % g, [P, ROW_TILES, PASS], F32)
+        def load_y(g, plane):
+            y_sb[g] = placed("y_sb%d" % g, plane, 0, [P, ROW_TILES, PASS], F32)
             nc.sync.dma_start(y_sb[g][:], y_rows[:, :, g * PASS : (g + 1) * PASS])
 
         def gather_whole(td):
             nc.vector.tensor_tensor(columns_k[:, td, :], planes[td][:].indirect(offsets[:]), norm_sb[:], MULT)
 
+        gather_whole(0)
+        raw = gather_plain(1, 1)
+        gather(1, 0)
+        scale(1, 1, raw)
         for td in range(2):
-            gather_whole(td)
             for g in range(PASSES):
                 turn_early(td, g, 3 + td * PASSES + g)
-        load_y(0, "plane0")
-        x_raw = reuse("plane1", "x_raw", [P, PACK, R], F32)
+        load_y(0, 0)
+        x_raw = placed("x_raw", 1, 0, [P, PACK, R], F32)
         nc.sync.dma_start(x_raw[:], xT.rearrange("(p t) r -> p t r", t=PACK))
-        make_weight(1)
         gather_whole(2)
-        turn_early(2, 0, 7)
-        load_y(1, "plane2")
+        load_y(1, 2)
+        raw = gather_plain(3, 1)
         gather(3, 0)
-        gather(3, 1)
-        rounded = {key: reuse("k_bf%d%d" % key, "k_bf%d%d" % key, [P, 2, P, PACK], BF16) for key in ((0, 0), (0, 1), (1, 1))}
-        k_codes[0, 0] = reuse("k_codes00", "k_codes00", [P, 2 * P], U32)[:]
+        scale(3, 1, raw)
+        rounded = {key: reuse("k_bf%d%d" % key, "k_bf%d%d" % key, [P, 2, P, PACK], BF16) for key in ((0, 0), (0, 1))}
+        rounded[1, 1] = placed("k_bf11", 1, 0, [P, 2, P, PACK], BF16)
         x_bf = reuse("norm_sb", "x_bf", [P, R, PACK], BF16)
         round_k(0, 0, nc.scalar.copy, rounded[0, 0][:])
         round_k(0, 1, nc.scalar.copy, rounded[0, 1][:])
         nc.vector.tensor_copy(x_bf[:].rearrange("p (c i) t -> p c t i", i=2), x_raw[:].rearrange("p t (c i) -> p c t i", i=2))
-        round_k(1, 1, nc.scalar.copy, rounded[1, 1][:])
-        quantize(x_codes[:], x_scales[:], x_bf[:].rearrange("p r t -> p (r t)"), E4M3)
-        round_k(1, 0, nc.vector.tensor_copy, reuse("norm_sb", "k_bf10", [P, 2, P, PACK], BF16)[:])
-        after_x = reuse("plane1", "after_x", [P, 2 * PASSES, D], U32)
-        kt_codes = after_x[:, 0:PASSES, :]
-        k_codes[0, 1] = after_x[:, PASSES, 0 : 2 * P]
-        for b in range(2):
-            k_codes[1, b] = after_x[:, PASSES + 1, b * 2 * P : (b + 1) * 2 * P]
-        y_banks0 = [turn_y(0, b, b) for b in range(2)]
-        y_banks1 = [turn_y(1, b, 6 + b) for b in range(2)]
+        round_k(1, 1, nc.scalar.copy, rounded[1, 1][:], slice(0, 3 * P // 4))
+        after_x = placed("after_x", 1, PASS, [P, 3 * PASS], U32)
+        kt_codes = [placed("kt_codes0", PACK - 1, 0, [P, D], U32), after_x[:, 2 * PASS : 3 * PASS]]
         for g in range(PASSES):
             for b in range(2):
-                quantize_k(g, b)
-                scores(g, b, 2 + 2 * g + b)
+                k_codes[g, b] = after_x[:, (2 * g + b) * 2 * P : (2 * g + b + 1) * 2 * P]
+        y_banks0 = [turn_y(0, b, b) for b in range(2)]
+        y_banks1 = [turn_y(1, 0, 6)]
+        quantize_k(0, 0)
+        quantize(x_codes[:], x_scales[:], x_bf[:].rearrange("p r t -> p (r t)"), E4M3)
+        scores(0, 0, 2)
+        round_k(1, 0, nc.vector.tensor_copy, reuse("norm_sb", "k_bf10", [P, 2, P, PACK], BF16)[:])
+        round_k(1, 1, nc.vector.tensor_copy, rounded[1, 1][:], slice(3 * P // 4, P))
+        quantize_k(0, 1)
+        scores(0, 1, 3)
+        for b in range(2):
+            quantize_k(1, b)
+            scores(1, b, 4 + b)
+        y_banks1.append(turn_y(1, 1, 2))
         quantize_kt(0, 0)
         quantize_kt(1, 0)
         for b in range(2):
             residual(0, b, y_banks0[b])
-        turn_late(0, (1,), 2)
-        turn_late(1, (0, 1), 3)
-        weigh(0, slice(0, R))
+        turn_late(0, (0, 1), 3)
+        turn_late(1, (0, 1), 4)
         residual(1, 0, y_banks1[0])
-        quantize_h(0, slice(0, R))
+        weigh(0, slice(0, R))
         residual(1, 1, y_banks1[1])
+        quantize_h(0, slice(0, R))
         quantize_kt(0, 1)
         sums = [bank(index, "sums") for index in (0, 1)]
         for j in range(ROW_TILES):

@@ -24,6 +24,7 @@ PASS = P * PACK
 PASSES = N // PASS
 ROW_TILES = R // P
 LIST_ROWS = 16
+SCALAR_SHARE = 3 * P // 4
 
 
 def tile_attend_gpq_nce_x_kernel(tc, xT, cb, norm, ts, y, wt, offs, out):
@@ -33,8 +34,8 @@ def tile_attend_gpq_nce_x_kernel(tc, xT, cb, norm, ts, y, wt, offs, out):
         shared = ctx.enter_context(tc.tile_pool(name="shared", bufs=1))
         ps = ctx.enter_context(tc.psum_pool(name="ps", bufs=1))
 
-        def bank(index, name, dtype=F32):
-            return ps.tile([P, PASS], dtype, name=name, tag="bank%d" % index)
+        def bank(index, name):
+            return ps.tile([P, PASS], F32, name=name, tag="bank%d" % index)
 
         def tiles(name, count, shape, dtype):
             return [sb.tile(shape, dtype, name="%s%d" % (name, i), align_bytes=64) for i in range(count)]
@@ -88,9 +89,10 @@ def tile_attend_gpq_nce_x_kernel(tc, xT, cb, norm, ts, y, wt, offs, out):
                 scale=ts_col[:, 1, t : t + 1],
             )
         for v, copy in enumerate((nc.vector.tensor_copy, nc.scalar.copy)):
-            norm_bank = spread(v, "norm_bank", [norm_col[:, 4 * v + c : 4 * v + c + 1] for c in range(4)])
+            norm_bank = spread(v, "norm_bank", [norm_col[:, PACK * v + c : PACK * v + c + 1] for c in range(PACK)])
             copy(
-                norm_sb[:].rearrange("q (s v c) -> q v s c", v=2, c=4)[:, v], norm_bank[:].rearrange("q (c s) -> q s c", c=4)
+                norm_sb[:].rearrange("q (s v c) -> q v s c", v=2, c=PACK)[:, v],
+                norm_bank[:].rearrange("q (c s) -> q s c", c=PACK),
             )
 
         planes.append(placed("plane3", PACK - 1, 0, [P, C], F32))
@@ -142,13 +144,13 @@ def tile_attend_gpq_nce_x_kernel(tc, xT, cb, norm, ts, y, wt, offs, out):
                 nc.tensor.transpose(turned[:, t * P : (t + 1) * P], gathered[g][:, td, t:PASS:PACK], identity[:])
             nc.scalar.copy(kt_bf[g, td // 2][:, td % 2], turned[:].rearrange("s (t p) -> s p t", t=PACK))
 
-        def turn_late(g, wanted, index):
+        def turn_late(g, index):
             turned = bank(index, "k_turned")
             for t in range(PACK):
                 words = k_bf[g, t // 2].rearrange("p t s d -> p t (s d)").bitcast(F32)
                 nc.tensor.transpose(turned[:, t * P : (t + 1) * P], words[:, t % 2, 1 : 2 * P : 2], identity[:])
             pairs = turned[:].bitcast(BF16).rearrange("s (t p e) -> s e p t", t=PACK, e=2)
-            for e in wanted:
+            for e in range(2):
                 nc.scalar.copy(kt_bf[g, 1][:, e], pairs[:, e])
 
         def quantize(codes, scales, values, fmt):
@@ -212,7 +214,7 @@ def tile_attend_gpq_nce_x_kernel(tc, xT, cb, norm, ts, y, wt, offs, out):
                 out=acc[:],
                 lhsT=h_codes[g][:, j * P : (j + 1) * P].bitcast(E5M2),
                 lhsT_scale=h_scales[g][:, j * P : (j + 1) * P],
-                rhs=kt_codes[g][:, :].bitcast(E4M3),
+                rhs=kt_codes[g][:, 0:D].bitcast(E4M3),
                 rhs_scale=kt_scales[g][:],
                 start=(g == 0),
                 stop=(g == PASSES - 1),
@@ -227,7 +229,8 @@ def tile_attend_gpq_nce_x_kernel(tc, xT, cb, norm, ts, y, wt, offs, out):
         def gather_whole(td):
             nc.vector.tensor_tensor(columns_k[:, td, :], planes[td][:].indirect(offsets[:]), norm_sb[:], MULT)
 
-        gather_whole(0)
+        for g in range(PASSES):
+            gather(0, g)
         raw = gather_plain(1, 1)
         gather(1, 0)
         scale(1, 1, raw)
@@ -248,7 +251,7 @@ def tile_attend_gpq_nce_x_kernel(tc, xT, cb, norm, ts, y, wt, offs, out):
         round_k(0, 0, nc.scalar.copy, rounded[0, 0][:])
         round_k(0, 1, nc.scalar.copy, rounded[0, 1][:])
         nc.vector.tensor_copy(x_bf[:].rearrange("p (c i) t -> p c t i", i=2), x_raw[:].rearrange("p t (c i) -> p c t i", i=2))
-        round_k(1, 1, nc.scalar.copy, rounded[1, 1][:], slice(0, 3 * P // 4))
+        round_k(1, 1, nc.scalar.copy, rounded[1, 1][:], slice(0, SCALAR_SHARE))
         after_x = placed("after_x", 1, PASS, [P, 3 * PASS], U32)
         kt_codes = [placed("kt_codes0", PACK - 1, 0, [P, D], U32), after_x[:, 2 * PASS : 3 * PASS]]
         for g in range(PASSES):
@@ -260,19 +263,19 @@ def tile_attend_gpq_nce_x_kernel(tc, xT, cb, norm, ts, y, wt, offs, out):
         quantize(x_codes[:], x_scales[:], x_bf[:].rearrange("p r t -> p (r t)"), E4M3)
         scores(0, 0, 2)
         round_k(1, 0, nc.vector.tensor_copy, reuse("norm_sb", "k_bf10", [P, 2, P, PACK], BF16)[:])
-        round_k(1, 1, nc.vector.tensor_copy, rounded[1, 1][:], slice(3 * P // 4, P))
+        round_k(1, 1, nc.vector.tensor_copy, rounded[1, 1][:], slice(SCALAR_SHARE, P))
         quantize_k(0, 1)
         scores(0, 1, 3)
         for b in range(2):
             quantize_k(1, b)
             scores(1, b, 4 + b)
-        y_banks1.append(turn_y(1, 1, 2))
         quantize_kt(0, 0)
         quantize_kt(1, 0)
         for b in range(2):
             residual(0, b, y_banks0[b])
-        turn_late(0, (0, 1), 3)
-        turn_late(1, (0, 1), 4)
+        turn_late(0, 2)
+        y_banks1.append(turn_y(1, 1, 3))
+        turn_late(1, 4)
         residual(1, 0, y_banks1[0])
         weigh(0, slice(0, R))
         residual(1, 1, y_banks1[1])
@@ -286,9 +289,9 @@ def tile_attend_gpq_nce_x_kernel(tc, xT, cb, norm, ts, y, wt, offs, out):
         quantize_h(1, slice(0, P))
         weigh(1, slice(P, R))
         quantize_h(1, slice(P, R))
+        pieces = 2
         for j in range(ROW_TILES):
             gradient(1, j, sums[j])
-            pieces = 2
             for i in range(pieces):
                 part = slice(i * P // pieces, (i + 1) * P // pieces)
                 cols = slice(i * D // pieces, (i + 1) * D // pieces)

@@ -200,9 +200,9 @@ def tile_attend_gpq_nce_x_kernel(tc, xT, cb, norm, ts, y, wt, offs, out):
 
         def weigh(g, rows):
             nc.vector.tensor_tensor(
-                h_bf[g][:, rows, :].rearrange("s (c i) t -> s c t i", i=2),
-                diff[g][:, :, rows].rearrange("s t (c i) -> s c t i", i=2),
-                weight[g][:, :, rows].rearrange("s t (c i) -> s c t i", i=2),
+                h_bf[g][:, rows, :].rearrange("s (c i) t -> s c t i", i=PACK),
+                diff[g][:, :, rows].rearrange("s t (c i) -> s c t i", i=PACK),
+                weight[g][:, :, rows].rearrange("s t (c i) -> s c t i", i=PACK),
                 MULT,
             )
 
@@ -250,7 +250,9 @@ def tile_attend_gpq_nce_x_kernel(tc, xT, cb, norm, ts, y, wt, offs, out):
         x_bf = reuse("norm_sb", "x_bf", [P, R, PACK], BF16)
         round_k(0, 0, nc.scalar.copy, rounded[0, 0][:])
         round_k(0, 1, nc.scalar.copy, rounded[0, 1][:])
-        nc.vector.tensor_copy(x_bf[:].rearrange("p (c i) t -> p c t i", i=2), x_raw[:].rearrange("p t (c i) -> p c t i", i=2))
+        nc.vector.tensor_copy(
+            x_bf[:].rearrange("p (c i) t -> p c t i", i=PACK), x_raw[:].rearrange("p t (c i) -> p c t i", i=PACK)
+        )
         round_k(1, 1, nc.scalar.copy, rounded[1, 1][:], slice(0, SCALAR_SHARE))
         after_x = placed("after_x", 1, PASS, [P, 3 * PASS], U32)
         kt_codes = [placed("kt_codes0", PACK - 1, 0, [P, D], U32), after_x[:, 2 * PASS : 3 * PASS]]

from contextlib import ExitStack

import concourse.mybir as mybir
from concourse.masks import make_identity

N, C, D, R = 1024, 2048, 512, 256
FLOPS = 2 * 2 * N * D * R

F32 = mybir.dt.float32
BF16 = mybir.dt.bfloat16
U32 = mybir.dt.uint32
U16 = mybir.dt.uint16
U8 = mybir.dt.uint8
E4M3 = mybir.dt.float8_e4m3fn_x4
E5M2 = mybir.dt.float8_e5m2_x4
MULT = mybir.AluOpType.mult
SUBTRACT = mybir.AluOpType.subtract
COPY = mybir.ActivationFunctionType.Copy
SIGMOID = mybir.ActivationFunctionType.Sigmoid

P = 128
PACK = 4
PASS = P * PACK
PASSES = N // PASS
ROW_TILES = R // P
LIST_ROWS = 16
SCALAR_SHARE = 3 * P // 4


def tile_attend_gpq_nce_x_kernel(tc, xT, cb, norm, ts, y, wt, offs, out):
    nc = tc.nc
    with ExitStack() as ctx:
        sb = ctx.enter_context(tc.tile_pool(name="sb", bufs=1))
        shared = ctx.enter_context(tc.tile_pool(name="shared", bufs=1))
        ps = ctx.enter_context(tc.psum_pool(name="ps", bufs=1))

        def bank(index, name):
            return ps.tile([P, PASS], F32, name=name, tag="bank%d" % index)

        def tiles(name, count, shape, dtype):
            return [sb.tile(shape, dtype, name="%s%d" % (name, i), align_bytes=64) for i in range(count)]

        def placed(name, plane, column, shape, dtype):
            return shared.tile(shape, dtype, name=name, align_bytes=64, offset=4 * (plane * C + column))

        offsets = sb.tile([P, N // LIST_ROWS], U16, name="offsets")
        norm_sb = sb.tile([P, N], F32, name="norm_sb", tag="norm_sb", align_bytes=64)
        planes = [placed("plane%d" % t, t, 0, [P, C], F32) for t in range(PACK - 1)]
        ts_col = sb.tile([P, PASSES, 2 * PACK], F32, name="ts_col")
        norm_col = placed("norm_col", PACK - 1, 0, [P, N // P], F32)
        wt_col = sb.tile([P, 2], F32, name="wt_col", tag="raw", align_bytes=64)

        cb_planes = cb.rearrange("(p t) c -> t p c", t=PACK)
        y_rows = y.rearrange("(j m) n -> m j n", m=P)
        nc.sync.dma_start(wt_col[:], wt.rearrange("(p e) o -> p (e o)", e=2))
        nc.sync.dma_start(ts_col[:, :, 0:PACK], ts[0:1, :].rearrange("o (g s t) -> s (o g) t", g=PASSES, t=PACK))
        nc.sync.dma_start(norm_col[:], norm[0:1, :].rearrange("o (s c) -> s (o c)", s=P))
        nc.sync.dma_start(planes[0][:], cb_planes[0])
        nc.sync.dma_start(offsets[:], offs)
        for t in range(1, PACK - 1):
            nc.sync.dma_start(planes[t][:], cb_planes[t])

        identity = sb.tile([P, P], F32, name="identity")
        make_identity(nc, identity[:])
        warm = sb.tile([P, 1], F32, name="warm")
        nc.scalar.activation(warm[:], identity[:, 0:1], SIGMOID)

        def spread(index, name, columns):
            turned = bank(index, name)
            for c, column in enumerate(columns):
                nc.tensor.transpose(turned[:, c * P : (c + 1) * P], column.to_broadcast([P, P]), identity[:])
            return turned

        wt_columns = [wt_col[:, e : e + 1] for e in range(2)]
        weight = tiles("weight", PASSES, [P, PACK, R], F32)
        wt_bank = spread(2, "wt_bank", wt_columns)
        nc.vector.tensor_tensor(
            weight[0][:].rearrange("s t (k e) -> s t k e", e=2),
            wt_bank[:, 0:R].rearrange("q (e k) -> q k e", e=2).unsqueeze(1).to_broadcast([P, PACK, P, 2]),
            ts_col[:, 0, 0:PACK].unsqueeze(2).unsqueeze(3).to_broadcast([P, PACK, P, 2]),
            MULT,
        )
        wt_bank = spread(7, "wt_bank", wt_columns)
        for t in range(PACK):
            nc.scalar.activation(
                weight[1][:, t, :].rearrange("q (k e) -> q k e", e=2),
                wt_bank[:, 0:R].rearrange("q (e k) -> q k e", e=2),
                COPY,
                scale=ts_col[:, 1, t : t + 1],
            )
        for v, copy in enumerate((nc.vector.tensor_copy, nc.scalar.copy)):
            norm_bank = spread(v, "norm_bank", [norm_col[:, PACK * v + c : PACK * v + c + 1] for c in range(PACK)])
            copy(
                norm_sb[:].rearrange("q (s v c) -> q v s c", v=2, c=PACK)[:, v],
                norm_bank[:].rearrange("q (c s) -> q s c", c=PACK),
            )

        planes.append(placed("plane3", PACK - 1, 0, [P, C], F32))
        nc.sync.dma_start(planes[PACK - 1][:], cb_planes[PACK - 1])

        def reuse(tag, name, shape, dtype):
            return sb.tile(shape, dtype, name=name, tag=tag, align_bytes=64)

        columns_k = sb.tile([P, PACK, N], F32, name="columns_k", align_bytes=64)
        gathered = [columns_k[:, :, g * PASS : (g + 1) * PASS] for g in range(PASSES)]
        k_bf = {}
        k_codes = {}
        k_scales = tiles("k_scales", PASSES, [P, PASS], U8)
        kt_bf = {key: reuse("kt_bf%d%d" % key, "kt_bf%d%d" % key, [P, 2, P, PACK], BF16) for key in ((0, 0), (0, 1), (1, 0), (1, 1))}
        kt_scales = tiles("kt_scales", PASSES, [P, D], U8)
        x_codes = sb.tile([P, R], U32, name="x_codes", align_bytes=64)
        x_scales = sb.tile([P, R], U8, name="x_scales", align_bytes=64)
        sig = [reuse("sig%d" % g, "sig%d" % g, [P, PACK, R], F32) for g in range(PASSES)]
        diff = tiles("diff", PASSES, [P, PACK, R], F32)
        h_bf = tiles("h_bf", PASSES, [P, R, PACK], BF16)
        h_codes = tiles("h_codes", PASSES, [P, R], U32)
        h_scales = tiles("h_scales", PASSES, [P, R], U8)
        result = tiles("result", ROW_TILES, [P, D], F32)

        def gather(td, g):
            columns = PASS // LIST_ROWS
            window = planes[td][:].indirect(offsets[:, g * columns : (g + 1) * columns])
            nc.vector.tensor_tensor(gathered[g][:, td, :], window, norm_sb[:, g * PASS : (g + 1) * PASS], MULT)

        def gather_plain(td, g):
            columns = PASS // LIST_ROWS
            raw = reuse("raw", "raw", [P, PASS], F32)
            nc.scalar.activation(raw[:], planes[td][:].indirect(offsets[:, g * columns : (g + 1) * columns]), COPY)
            return raw

        def scale(td, g, raw):
            nc.vector.tensor_tensor(gathered[g][:, td, :], raw[:], norm_sb[:, g * PASS : (g + 1) * PASS], MULT)

        def round_k(g, b, copy, rounded, part=slice(0, P)):
            k_bf[g, b] = rounded
            copy(
                k_bf[g, b].rearrange("p t s d -> p s d t")[:, part],
                gathered[g].rearrange("p d (s t) -> p s d t", t=PACK)[:, part, :, 2 * b : 2 * b + 2],
            )

        def turn_early(td, g, index):
            turned = bank(index, "k_turned")
            for t in range(PACK):
                nc.tensor.transpose(turned[:, t * P : (t + 1) * P], gathered[g][:, td, t:PASS:PACK], identity[:])
            nc.scalar.copy(kt_bf[g, td // 2][:, td % 2], turned[:].rearrange("s (t p) -> s p t", t=PACK))

        def turn_late(g, index):
            turned = bank(index, "k_turned")
            for t in range(PACK):
                words = k_bf[g, t // 2].rearrange("p t s d -> p t (s d)").bitcast(F32)
                nc.tensor.transpose(turned[:, t * P : (t + 1) * P], words[:, t % 2, 1 : 2 * P : 2], identity[:])
            pairs = turned[:].bitcast(BF16).rearrange("s (t p e) -> s e p t", t=PACK, e=2)
            for e in range(2):
                nc.scalar.copy(kt_bf[g, 1][:, e], pairs[:, e])

        def quantize(codes, scales, values, fmt):
            nc.vector.quantize_mx(out=codes.bitcast(fmt), scales=scales, in_=values)

        def quantize_kt(g, u):
            half = slice(u * D // 2, (u + 1) * D // 2)
            quantize(kt_codes[g][:, half], kt_scales[g][:, half], kt_bf[g, u][:].rearrange("s e p t -> s (e p t)"), E4M3)

        def quantize_k(g, b):
            cols = slice(2 * b * P, 2 * (b + 1) * P)
            quantize(k_codes[g, b], k_scales[g][:, cols], k_bf[g, b].rearrange("p t s d -> p (t s d)"), E4M3)

        def turn_y(g, b, index):
            turned = bank(index, "y_turned")
            for t in (2 * b, 2 * b + 1):
                for j in range(ROW_TILES):
                    first = (t % 2) * R + j * P
                    nc.tensor.transpose(turned[:, first : first + P], y_sb[g][:, j, t:PASS:PACK], identity[:])
            return turned

        def scores(g, b, index):
            acc = bank(index, "score")
            for t in (2 * b, 2 * b + 1):
                cols = slice(t * P, (t + 1) * P)
                nc.tensor.matmul_mx(
                    out=acc[:, (t % 2) * R : (t % 2 + 1) * R],
                    lhsT=k_codes[g, b][:, (t % 2) * P : (t % 2 + 1) * P].bitcast(E4M3),
                    lhsT_scale=k_scales[g][:, cols],
                    rhs=x_codes[:].bitcast(E4M3),
                    rhs_scale=x_scales[:],
                    start=True,
                    stop=True,
                )
            for t in (2 * b, 2 * b + 1):
                nc.scalar.activation(
                    sig[g][:, t, :], acc[:, (t % 2) * R : (t % 2 + 1) * R], SIGMOID, scale=ts_col[:, g, t : t + 1]
                )

        def residual(g, b, y_turned):
            nc.vector.tensor_tensor(
                diff[g][:, 2 * b : 2 * b + 2, :].rearrange("s t r -> s (t r)"),
                sig[g][:, 2 * b : 2 * b + 2, :].rearrange("s t r -> s (t r)"),
                y_turned[:],
                SUBTRACT,
            )

        def weigh(g, rows):
            nc.vector.tensor_tensor(
                h_bf[g][:, rows, :].rearrange("s (c i) t -> s c t i", i=PACK),
                diff[g][:, :, rows].rearrange("s t (c i) -> s c t i", i=PACK),
                weight[g][:, :, rows].rearrange("s t (c i) -> s c t i", i=PACK),
                MULT,
            )

        def quantize_h(g, rows):
            quantize(h_codes[g][:, rows], h_scales[g][:, rows], h_bf[g][:, rows, :].rearrange("s m t -> s (m t)"), E5M2)

        def gradient(g, j, acc):
            nc.tensor.matmul_mx(
                out=acc[:],
                lhsT=h_codes[g][:, j * P : (j + 1) * P].bitcast(E5M2),
                lhsT_scale=h_scales[g][:, j * P : (j + 1) * P],
                rhs=kt_codes[g][:, 0:D].bitcast(E4M3),
                rhs_scale=kt_scales[g][:],
                start=(g == 0),
                stop=(g == PASSES - 1),
            )

        y_sb = {}

        def load_y(g, plane):
            y_sb[g] = placed("y_sb%d" % g, plane, 0, [P, ROW_TILES, PASS], F32)
            nc.sync.dma_start(y_sb[g][:], y_rows[:, :, g * PASS : (g + 1) * PASS])

        def gather_whole(td):
            nc.vector.tensor_tensor(columns_k[:, td, :], planes[td][:].indirect(offsets[:]), norm_sb[:], MULT)

        for g in range(PASSES):
            gather(0, g)
        raw = gather_plain(1, 1)
        gather(1, 0)
        scale(1, 1, raw)
        for td in range(2):
            for g in range(PASSES):
                turn_early(td, g, 3 + td * PASSES + g)
        load_y(0, 0)
        x_raw = placed("x_raw", 1, 0, [P, PACK, R], F32)
        nc.sync.dma_start(x_raw[:], xT.rearrange("(p t) r -> p t r", t=PACK))
        gather_whole(2)
        load_y(1, 2)
        raw = gather_plain(3, 1)
        gather(3, 0)
        scale(3, 1, raw)
        rounded = {key: reuse("k_bf%d%d" % key, "k_bf%d%d" % key, [P, 2, P, PACK], BF16) for key in ((0, 0), (0, 1))}
        rounded[1, 1] = placed("k_bf11", 1, 0, [P, 2, P, PACK], BF16)
        x_bf = reuse("norm_sb", "x_bf", [P, R, PACK], BF16)
        round_k(0, 0, nc.scalar.copy, rounded[0, 0][:])
        round_k(0, 1, nc.scalar.copy, rounded[0, 1][:])
        nc.vector.tensor_copy(
            x_bf[:].rearrange("p (c i) t -> p c t i", i=PACK), x_raw[:].rearrange("p t (c i) -> p c t i", i=PACK)
        )
        round_k(1, 1, nc.scalar.copy, rounded[1, 1][:], slice(0, SCALAR_SHARE))
        after_x = placed("after_x", 1, PASS, [P, 3 * PASS], U32)
        kt_codes = [placed("kt_codes0", PACK - 1, 0, [P, D], U32), after_x[:, 2 * PASS : 3 * PASS]]
        for g in range(PASSES):
            for b in range(2):
                k_codes[g, b] = after_x[:, (2 * g + b) * 2 * P : (2 * g + b + 1) * 2 * P]
        y_banks0 = [turn_y(0, b, b) for b in range(2)]
        y_banks1 = [turn_y(1, 0, 6)]
        quantize_k(0, 0)
        quantize(x_codes[:], x_scales[:], x_bf[:].rearrange("p r t -> p (r t)"), E4M3)
        scores(0, 0, 2)
        round_k(1, 0, nc.vector.tensor_copy, reuse("norm_sb", "k_bf10", [P, 2, P, PACK], BF16)[:])
        round_k(1, 1, nc.vector.tensor_copy, rounded[1, 1][:], slice(SCALAR_SHARE, P))
        quantize_k(0, 1)
        scores(0, 1, 3)
        for b in range(2):
            quantize_k(1, b)
            scores(1, b, 4 + b)
        quantize_kt(0, 0)
        quantize_kt(1, 0)
        for b in range(2):
            residual(0, b, y_banks0[b])
        turn_late(0, 2)
        y_banks1.append(turn_y(1, 1, 3))
        turn_late(1, 4)
        residual(1, 0, y_banks1[0])
        weigh(0, slice(0, R))
        residual(1, 1, y_banks1[1])
        quantize_h(0, slice(0, R))
        quantize_kt(0, 1)
        sums = [bank(index, "sums") for index in (0, 1)]
        for j in range(ROW_TILES):
            gradient(0, j, sums[j])
        weigh(1, slice(0, P))
        quantize_kt(1, 1)
        quantize_h(1, slice(0, P))
        weigh(1, slice(P, R))
        quantize_h(1, slice(P, R))
        pieces = 2
        for j in range(ROW_TILES):
            gradient(1, j, sums[j])
            for i in range(pieces):
                part = slice(i * P // pieces, (i + 1) * P // pieces)
                cols = slice(i * D // pieces, (i + 1) * D // pieces)
                (nc.scalar.copy, nc.vector.tensor_copy)[j](
                    result[j][:, cols].rearrange("m (p d) -> m p d", d=PACK),
                    sums[j][:].rearrange("m (d p) -> m p d", d=PACK)[:, part, :],
                )
                nc.sync.dma_start(out[j * P : (j + 1) * P, cols], result[j][:, cols])
